import numpy as np
import ml_dtypes


def mxq(x, axis, fmt="e4m3"):
    dtype, down = {"e4m3": (ml_dtypes.float8_e4m3fn, 7), "e5m2": (ml_dtypes.float8_e5m2, 14)}[fmt]
    v = np.moveaxis(np.asarray(x, np.float32).astype(ml_dtypes.bfloat16).astype(np.float64), axis, -1)
    blocks = v.reshape(v.shape[:-1] + (-1, 32))
    amax = np.abs(blocks).max(-1, keepdims=True)
    byte = np.maximum(np.where(amax > 0, np.frexp(amax)[1] - 1 + 127, 0) - down, 1)
    scale = np.exp2(byte - 127.0)
    codes = (blocks / scale).astype(np.float32).astype(dtype).astype(np.float64)
    return np.moveaxis((codes * scale).reshape(v.shape), -1, axis)


WIDE = False


def mx_kscale(k):
    if not WIDE:
        return np.ones(k)
    levels = np.array([10, -10, 5, -5, 0])
    if k % 512:
        return np.exp2(np.random.permutation(np.resize(levels, k // 32))).repeat(32)
    a = np.empty((k // 512, 16))
    for p in range(k // 512):
        a[p, :8] = np.random.permutation(np.resize(levels, 8))
        for g in range(8):
            far = levels[np.abs(levels - a[p, g]) >= 10]
            a[p, g + 8] = far[np.random.randint(len(far))]
    return np.exp2(a.ravel()).repeat(32)


def f64(x):
    return np.asarray(x).astype(np.float64)


def striped(idx):
    return np.tile(idx.reshape(-1, 16).T, (8, 1)).astype(np.uint16)


def unstriped(offs):
    return offs[:16].T.reshape(-1).astype(np.int64)


E2M1 = np.array([0.0, 0.5, 1.0, 1.5, 2.0, 3.0, 4.0, 6.0, -0.0, -0.5, -1.0, -1.5, -2.0, -3.0, -4.0, -6.0])


def pack_weight(w, fmt):
    k, n = w.shape
    w = f64(np.asarray(w, np.float32).astype(ml_dtypes.bfloat16)).reshape(k // 32, 32, n)
    amax = np.abs(w).max(1)
    if fmt == "e4m3":
        byte = np.frexp(amax)[1] - 1 + 127 - 7
    else:
        mant, ex = np.frexp(amax / 6.0)
        byte = np.where(mant > 0.5, ex, ex - 1) + 127
    byte = np.clip(np.where(amax > 0, byte, 1), 1, 254)
    scaled = (w * np.exp2(127.0 - byte)[:, None, :]).reshape(k, n).astype(np.float32)
    by_word = np.ascontiguousarray(scaled.reshape(k // 512, 128, 4, n).transpose(0, 1, 3, 2))
    if fmt == "e4m3":
        words = by_word.astype(ml_dtypes.float8_e4m3fn).view(np.uint8)
    else:
        c = by_word.astype(ml_dtypes.float4_e2m1fn).view(np.uint8) & 0xF
        words = (c[..., 0::2] | (c[..., 1::2] << 4)).reshape(k // 512, 128, 2 * n)
    return np.ascontiguousarray(words), np.ascontiguousarray(byte.astype(np.uint8).reshape(k // 512, 16, n))


def unpack_weight(words, scales, fmt):
    g, _, n = scales.shape
    words = np.ascontiguousarray(words).reshape(g, 128, n, -1)
    if fmt == "e4m3":
        vals = words.view(ml_dtypes.float8_e4m3fn).astype(np.float64)
    else:
        nib = np.empty((g, 128, n, 4), np.uint8)
        nib[..., 0::2] = words & 0xF
        nib[..., 1::2] = words >> 4
        vals = E2M1[nib]
    vals = vals * np.repeat(np.exp2(scales.astype(np.float64) - 127.0), 8, axis=1)[..., None]
    return vals.transpose(0, 1, 3, 2).reshape(g * 512, n)


def gelu(v):
    return 0.5 * v * (1.0 + np.tanh(np.sqrt(2.0 / np.pi) * (v + 0.044715 * v**3)))


def bf(x):
    return np.asarray(x, np.float32).astype(ml_dtypes.bfloat16)


def planes(Y):
    n, m = Y.shape
    b = f64(bf(Y)).reshape(n // 32, 32, m)
    amax = np.abs(b).max(1)
    byte = np.clip(np.where(amax > 0, np.frexp(amax)[1] - 1 + 127 - 7, 1), 1, 254)
    codes = (b * np.exp2(127.0 - byte)[:, None, :]).reshape(n, m).astype(np.float32).astype(ml_dtypes.float8_e4m3fn).view(np.uint8)
    words = codes.reshape(n // 512, 128, 4, m).transpose(0, 1, 3, 2)
    return np.ascontiguousarray(words), np.ascontiguousarray(byte.astype(np.uint8).reshape(n // 512, 16, m))


K, T, S, H, T2, P, N = 1024, 4096, 1024, 512, 2048, 1024, 384


def setup_inputs():
    n = np.random.standard_normal
    s = mx_kscale(K)[:, None]
    u = mx_kscale(H)[:, None]
    d = {}
    d["tab_words"], d["tab_scales"] = pack_weight(n((K, T)) * s, "e4m3")
    d["offs"] = striped(np.random.permutation(T)[:S])
    d["offs2"] = striped(np.random.permutation(T2)[:S])
    d["offs3"] = striped(np.random.permutation(T2)[:P])
    d["w1"] = (n((K, H)) / K ** 0.5 / s * u.T).astype(np.float32)
    d["w2_words"], d["w2_scales"] = pack_weight(n((K, H)) / K ** 0.5 / s * u.T, "e2m1")
    d["season"] = np.exp(0.4 * n((H, S))).astype(np.float32)
    d["wgs"] = np.exp(0.3 * n((128, S))).astype(np.float32)
    d["page0"] = (n((H, T2)) * u).astype(np.float32)
    d["tare"] = ((0.6 + 0.5 * n(H)) * u[:, 0]).astype(np.float32)
    d["w3"] = (n((H, N)) / H ** 0.5 / u).astype(np.float32)
    d["w4_words"], d["w4_scales"] = pack_weight(1.4 * n((H, N)) / H ** 0.5 / u, "e4m3")
    return d


def reference(tab_words, tab_scales, offs, offs2, offs3, w1, w2_words, w2_scales, season, wgs, page0, tare, w3, w4_words, w4_scales):
    v = unpack_weight(tab_words, tab_scales, "e4m3")[:, unstriped(offs)]
    a = mxq(f64(w1), 0, "e4m3").T @ v
    b = unpack_weight(w2_words, w2_scales, "e2m1").T @ v
    h = np.maximum(a, b) * f64(season)
    page = f64(page0).copy()
    page[:, unstriped(offs2)] = np.tile(f64(wgs), (H // 128, 1)) * h
    x = np.abs(page[:, unstriped(offs3)]) - f64(tare)[:, None]
    e = mxq(f64(w3), 0, "e4m3").T @ mxq(x, 0, "e4m3")
    f = unpack_weight(w4_words, w4_scales, "e4m3").T @ mxq(h, 0, "e4m3")
    y = e - np.tanh(f)
    words, scales = planes(page)
    return y, page, words, scales

@@ -1,0 +1,338 @@
+from contextlib import ExitStack
+
+import concourse.mybir as mybir
+
+K, T, S, H, T2, N = 1024, 4096, 1024, 512, 2048, 384
+FLOPS = 2 * (2 * K * H * S + 2 * H * N * S)
+
+F32 = mybir.dt.float32
+BF16 = mybir.dt.bfloat16
+I32 = mybir.dt.int32
+U32 = mybir.dt.uint32
+U16 = mybir.dt.uint16
+U8 = mybir.dt.uint8
+FP8X4 = mybir.dt.float8_e4m3fn_x4
+FP4X4 = mybir.dt.float4_e2m1fn_x4
+ALU = mybir.AluOpType
+ACT = mybir.ActivationFunctionType
+
+P = 128
+PACK = 4
+PASSES = K // (P * PACK)
+HALF = 512
+HALVES = S // HALF
+LCOL = HALF // 16
+QUADS = 4
+CHUNK = 512
+CHUNKS = T2 // CHUNK
+NT = N // P
+
+
+def tile_list_penguin_pair_page_kernel(
+    tc, tab_words, tab_scales, offs, offs2, offs3, w1, w2_words, w2_scales, season, wgs, page0, tare, w3,
+    w4_words, w4_scales, out_0, out_1, out_2, out_3,
+):
+    nc = tc.nc
+    with ExitStack() as ctx:
+        lists = ctx.enter_context(tc.tile_pool(name="lists", bufs=1))
+        keep = ctx.enter_context(tc.tile_pool(name="keep", bufs=1))
+        ring = ctx.enter_context(tc.tile_pool(name="ring", bufs=3))
+        psum = ctx.enter_context(tc.psum_pool(name="psum", bufs=2))
+
+        idx = lists.tile([P, S // 16], U16, name="idx")
+        idx2 = lists.tile([P, S // 16], U16, name="idx2")
+        idx3 = lists.tile([P, S // 16], U16, name="idx3")
+
+        def kept(shape, dtype, name):
+            return keep.tile(shape, dtype, name=name, tag=name, align_bytes=64)
+
+        v_words = [[kept([P, HALF], U32, f"vw{a}{h}") for h in range(HALVES)] for a in range(PASSES)]
+        v_rows = kept([P, S], U8, "v_rows")
+        v_scales = [kept([P, S], U8, f"vs{a}") for a in range(PASSES)]
+        w1_codes = [kept([P, H], U32, f"w1c{a}") for a in range(PASSES)]
+        w1_scales = [kept([P, H], U8, f"w1s{a}") for a in range(PASSES)]
+        w2_codes = kept([P, PASSES, 2 * H], U8, "w2c")
+        w2_sc = kept([P, PASSES, H], U8, "w2s")
+        w3_raw = kept([P, PACK, N], F32, "w3raw")
+        w3_codes = kept([P, N], U32, "w3c")
+        w3_scales = kept([P, N], U8, "w3s")
+        w4_codes = kept([P, N], I32, "w4c")
+        w4_sc = kept([P, N], U8, "w4s")
+        tare_t = kept([P, PACK], F32, "tare_t")
+        pages = [kept([P, T2], F32, f"page{t}") for t in range(PACK)]
+        sea = [[kept([P, HALF], F32, f"sea{t}{h}") for h in range(HALVES)] for t in range(PACK)]
+        wg = [[kept([P, HALF], F32, f"wg{t}{h}") for h in range(HALVES)] for t in range(PACK)]
+        hf = [kept([P, PACK, HALF], F32, f"hf{h}") for h in range(HALVES)]
+
+        season_v = season.rearrange("(p t) j -> t p j", t=PACK)
+        wgs_v = wgs.rearrange("(m t) j -> t m j", t=PACK)
+        page_v = page0.rearrange("(p t) m -> t p m", t=PACK)
+        out1_v = out_1.rearrange("(p t) m -> t p m", t=PACK)
+
+        def load_season(t, h):
+            nc.sync.dma_start(out=sea[t][h][:], in_=season_v[t][:, h * HALF : (h + 1) * HALF])
+
+        def load_wgs(t, h):
+            for q in (0, 2, 1, 3):
+                nc.sync.dma_start(out=wg[t][h][32 * q : 32 * q + 32, :], in_=wgs_v[t][:, h * HALF : (h + 1) * HALF])
+
+        def load_page(t):
+            nc.sync.dma_start(out=pages[t][:], in_=page_v[t])
+
+        with tc.tile_pool(name="head", bufs=1) as head:
+            tw = [head.tile([P, T], I32, name=f"tw{a}", align_bytes=64) for a in range(PASSES)]
+            ts = head.tile([P, T], U8, name="ts", align_bytes=64)
+            w1_raw = [head.tile([P, PACK, H], F32, name=f"w1raw{a}", align_bytes=64) for a in range(PASSES)]
+            w1_bf = [head.tile([P, H, PACK], BF16, name=f"w1bf{a}", align_bytes=64) for a in range(PASSES)]
+            w2_raw = head.tile([P, PASSES, 2 * H], U8, name="w2raw", align_bytes=64)
+            w2s_raw = head.tile([P, PASSES, H], U8, name="w2sraw", align_bytes=64)
+
+            nc.vector.memset(w2s_raw[:].rearrange("p a c -> p (a c)").bitcast(I32), 0)
+            nc.vector.memset(ts[32:64, :].bitcast(I32), 0)
+            nc.vector.memset(ts[64:128, :].bitcast(I32), 0)
+            for a in range(PASSES):
+                nc.vector.memset(v_scales[a][:].bitcast(I32), 0)
+            nc.vector.memset(w4_sc[:].bitcast(I32), 0)
+
+            w1_v = w1.rearrange("(a p i) c -> a p i c", a=PASSES, i=PACK)
+            tw_v = tab_words.rearrange("a p t i -> a p (t i)")
+            nc.sync.dma_start(idx[:], offs)
+            nc.sync.dma_start(
+                out=ts[0:32, :].bitcast(I32), in_=tab_scales.rearrange("a q t -> (a q) t").bitcast(I32)
+            )
+            nc.sync.dma_start(out=w1_raw[0][:], in_=w1_v[0])
+            nc.sync.dma_start(out=w2_raw[:].bitcast(I32), in_=w2_words.rearrange("a p c -> p a c").bitcast(I32))
+            nc.sync.dma_start(out=w1_raw[1][:], in_=w1_v[1])
+            for a in range(PASSES):
+                nc.sync.dma_start(out=tw[a][:], in_=tw_v[a].bitcast(I32))
+            for q in range(QUADS):
+                nc.gpsimd.dma_start(
+                    out=w2s_raw[32 * q : 32 * q + 4, :, :].bitcast(I32),
+                    in_=w2_scales[:, 4 * q : 4 * q + 4, :].rearrange("a r c -> r a c").bitcast(I32),
+                )
+
+            load_season(0, 0)
+            nc.sync.dma_start(idx2[:], offs2)
+            load_season(0, 1)
+            load_wgs(0, 0)
+            load_page(0)
+            load_wgs(0, 1)
+            nc.sync.dma_start(idx3[:], offs3)
+            nc.sync.dma_start(out=w3_raw[:], in_=w3.rearrange("(p i) c -> p i c", i=PACK))
+            nc.sync.dma_start(out=tare_t[:], in_=tare.rearrange("(p t) -> p t", t=PACK))
+            load_season(1, 0)
+            load_season(1, 1)
+            load_wgs(1, 0)
+            load_page(1)
+            load_wgs(1, 1)
+            for t in (2, 3):
+                for h in range(HALVES):
+                    load_season(t, h)
+            nc.sync.dma_start(out=w4_codes[:], in_=w4_words.rearrange("a p c i -> p (a c i)").bitcast(I32))
+            for t in (2, 3):
+                load_wgs(t, 0)
+                load_page(t)
+                load_wgs(t, 1)
+
+            nc.vector.tensor_copy(v_rows[:], ts[:].indirect(idx[:]))
+            for a in range(PASSES):
+                for q in range(QUADS):
+                    first = 16 * a + 4 * q
+                    nc.gpsimd.dma_start(
+                        out=v_scales[a][32 * q : 32 * q + 4, :].bitcast(I32),
+                        in_=v_rows[first : first + 4, :].bitcast(I32),
+                    )
+            for q in range(QUADS):
+                nc.gpsimd.dma_start(
+                    out=w4_sc[32 * q : 32 * q + 4, :].bitcast(I32), in_=w4_scales[0, 4 * q : 4 * q + 4, :].bitcast(I32)
+                )
+
+            for a in range(PASSES):
+                nc.vector.tensor_copy(
+                    out=w2_codes[:, a, :].rearrange("p (t m b) -> p t m b", t=PACK, b=2),
+                    in_=w2_raw[:, a, :].rearrange("p (m t b) -> p t m b", t=PACK, b=2),
+                )
+            nc.vector.tensor_copy(
+                out=w2_sc[:].rearrange("p a (t m) -> p a t m", t=PACK),
+                in_=w2s_raw[:].rearrange("p a (m t) -> p a t m", t=PACK),
+            )
+            for a in range(PASSES):
+                nc.scalar.copy(
+                    out=w1_bf[a][:].rearrange("p (t m) i -> p m t i", t=PACK),
+                    in_=w1_raw[a][:].rearrange("p i (m t) -> p m t i", t=PACK),
+                )
+                nc.vector.quantize_mx(
+                    out=w1_codes[a][:].bitcast(FP8X4), scales=w1_scales[a][:],
+                    in_=w1_bf[a][:].rearrange("p c i -> p (c i)"),
+                )
+            for a in range(PASSES):
+                for h in range(HALVES):
+                    nc.vector.tensor_copy(
+                        v_words[a][h][:], tw[a][:].bitcast(U32).indirect(idx[:, h * LCOL : (h + 1) * LCOL])
+                    )
+
+        tail = ctx.enter_context(tc.tile_pool(name="tail", bufs=1))
+
+        def late(shape, dtype, name):
+            return tail.tile(shape, dtype, name=name, align_bytes=64)
+
+        page_pairs = [late([P, 2, CHUNK, 2], BF16, f"pp{c}") for c in range(CHUNKS)]
+        page_codes = [late([P, CHUNK], U32, f"pc{c}") for c in range(CHUNKS)]
+        page_scales = late([P, T2], U8, "ps")
+        got = [late([P, PACK, HALF], F32, f"got{h}") for h in range(HALVES)]
+        x_pairs = [late([P, 2, HALF, 2], BF16, f"xp{h}") for h in range(HALVES)]
+        ys = [[late([P, HALF], F32, f"y{h}{n}") for n in range(NT)] for h in range(HALVES)]
+
+        def prepare_w3():
+            w3_bf = keep.tile([P, N, PACK], BF16, name="w3bf", tag="wg00", align_bytes=64)
+            nc.scalar.copy(out=w3_bf[:], in_=w3_raw[:].rearrange("p i c -> p c i"))
+            for c0, c1 in ((0, 256), (256, N)):
+                nc.vector.quantize_mx(
+                    out=w3_codes[:, c0:c1].bitcast(FP8X4), scales=w3_scales[:, c0:c1],
+                    in_=w3_bf[:, c0:c1, :].rearrange("p c i -> p (c i)"),
+                )
+
+        def negate_tare():
+            neg = keep.tile([P, PACK], F32, name="neg_tare", tag="wg01", align_bytes=64)
+            nc.vector.tensor_scalar(neg[:], tare_t[:], -1.0, None, ALU.mult)
+            return neg
+
+        def products(t, h):
+            cols = slice(P * t, P * (t + 1))
+            jc = slice(HALF * h, HALF * (h + 1))
+            b_ps = psum.tile([P, HALF], F32, name="b_ps")
+            a_ps = psum.tile([P, HALF], F32, name="a_ps", bufs=3)
+            for a in range(PASSES):
+                nc.tensor.matmul_mx(
+                    out=b_ps[:], lhsT=w2_codes[:, a, 2 * P * t : 2 * P * (t + 1)].bitcast(FP4X4),
+                    lhsT_scale=w2_sc[:, a, cols], rhs=v_words[a][h][:].bitcast(FP8X4), rhs_scale=v_scales[a][:, jc],
+                    start=(a == 0), stop=(a == PASSES - 1),
+                )
+            for a in range(PASSES):
+                nc.tensor.matmul_mx(
+                    out=a_ps[:], lhsT=w1_codes[a][:, cols].bitcast(FP8X4), lhsT_scale=w1_scales[a][:, cols],
+                    rhs=v_words[a][h][:].bitcast(FP8X4), rhs_scale=v_scales[a][:, jc],
+                    start=(a == 0), stop=(a == PASSES - 1),
+                )
+            b_sb = ring.tile([P, HALF], F32, name="b_sb")
+            nc.scalar.copy(out=b_sb[:], in_=b_ps[:])
+            return a_ps, b_sb
+
+        def larger(a_ps, b_sb):
+            big = ring.tile([P, HALF], F32, name="big")
+            nc.vector.tensor_tensor(big[:], a_ps[:], b_sb[:], ALU.max)
+            return big
+
+        def seasoned(t, h, big):
+            nc.vector.tensor_tensor(hf[h][:, t, :], big[:], sea[t][h][:], ALU.mult)
+
+        def place(t, h):
+            nc.vector.tensor_tensor(
+                pages[t][:].indirect(idx2[:, h * LCOL : (h + 1) * LCOL]), hf[h][:, t, :], wg[t][h][:], ALU.mult
+            )
+
+        def round_page(t, chunks):
+            for c in chunks:
+                nc.scalar.copy(out=page_pairs[c][:, t // 2, :, t % 2], in_=pages[t][:, c * CHUNK : (c + 1) * CHUNK])
+
+        def read_page(t, neg_tare):
+            for h in range(HALVES):
+                nc.vector.tensor_copy(got[h][:, t, :], pages[t][:].indirect(idx3[:, h * LCOL : (h + 1) * LCOL]))
+                nc.scalar.activation(got[h][:, t, :], got[h][:, t, :], ACT.Abs)
+                nc.scalar.activation(
+                    x_pairs[h][:, t // 2, :, t % 2], got[h][:, t, :], ACT.Identity, bias=neg_tare[:, t : t + 1]
+                )
+
+        def quantise(name, grouped):
+            codes = late([P, HALF], U32, name + "c")
+            scales = late([P, HALF], U8, name + "s")
+            nc.vector.quantize_mx(out=codes[:].bitcast(FP8X4), scales=scales[:], in_=grouped)
+            return codes, scales
+
+        def weave(pairs):
+            woven = tail.tile([P, HALF, 2], I32, name="woven", bufs=3, align_bytes=64)
+            nc.vector.tensor_copy(
+                out=woven[:],
+                in_=pairs[:].rearrange("p u m e -> p (u m e)").bitcast(I32).rearrange("p (u m) -> p m u", u=2),
+            )
+            return woven[:].rearrange("p m u -> p (m u)").bitcast(BF16)
+
+        def round_h(h):
+            h_bf = late([P, HALF, PACK], BF16, f"hbf{h}")
+            nc.scalar.copy(out=h_bf[:], in_=hf[h][:].rearrange("p t j -> p j t"))
+            return h_bf
+
+        def tanh_part(h, h_bf):
+            codes, scales = quantise(f"hq{h}", h_bf[:].rearrange("p j t -> p (j t)"))
+            for n in range(NT):
+                cols = slice(P * n, P * (n + 1))
+                f_ps = psum.tile([P, HALF], F32, name="f_ps", bufs=1)
+                nc.tensor.matmul_mx(
+                    out=f_ps[:], lhsT=w4_codes[:, cols].bitcast(FP8X4), lhsT_scale=w4_sc[:, cols],
+                    rhs=codes[:].bitcast(FP8X4), rhs_scale=scales[:], start=True, stop=True,
+                )
+                nc.scalar.activation(ys[h][n][:], f_ps[:], ACT.Tanh)
+
+        def finish(h):
+            codes, scales = quantise(f"xq{h}", weave(x_pairs[h]))
+            for n in range(NT):
+                cols = slice(P * n, P * (n + 1))
+                e_ps = psum.tile([P, HALF], F32, name="e_ps")
+                nc.tensor.matmul_mx(
+                    out=e_ps[:], lhsT=w3_codes[:, cols].bitcast(FP8X4), lhsT_scale=w3_scales[:, cols],
+                    rhs=codes[:].bitcast(FP8X4), rhs_scale=scales[:], start=True, stop=True,
+                )
+                nc.vector.tensor_tensor(ys[h][n][:], e_ps[:], ys[h][n][:], ALU.subtract)
+                nc.sync.dma_start(out=out_0[cols, HALF * h : HALF * (h + 1)], in_=ys[h][n][:])
+
+        def planes(c):
+            cols = slice(c * CHUNK, (c + 1) * CHUNK)
+            nc.vector.quantize_mx(
+                out=page_codes[c][:].bitcast(FP8X4), scales=page_scales[:, cols], in_=weave(page_pairs[c])
+            )
+            nc.sync.dma_start(
+                out=out_2.rearrange("g p m t -> p (g m t)").bitcast(I32)[:, cols], in_=page_codes[c][:].bitcast(I32)
+            )
+
+        units = [(t, h) for t in range(PACK) for h in range(HALVES)]
+        sums = {}
+        bigs = {}
+        h_bfs = []
+
+        def step(n):
+            if n + 2 < len(units):
+                sums[n + 2] = products(*units[n + 2])
+            if n + 1 < len(units):
+                bigs[n + 1] = larger(*sums[n + 1])
+            if 0 <= n < len(units):
+                seasoned(*units[n], bigs[n])
+                if units[n][0] == PACK - 1:
+                    h_bfs.append(round_h(units[n][1]))
+
+        sums[0] = products(*units[0])
+        step(-1)
+        step(0)
+        step(1)
+        for n, (t, h) in enumerate(units):
+            place(t, h)
+            step(n + 2)
+            if n == 0:
+                prepare_w3()
+            if n == 1:
+                neg_tare = negate_tare()
+            if h == HALVES - 1:
+                nc.sync.dma_start(out=out1_v[t], in_=pages[t][:])
+                read_page(t, neg_tare)
+                if t < PACK - 1:
+                    round_page(t, range(CHUNKS))
+        for h in range(HALVES):
+            tanh_part(h, h_bfs[h])
+            round_page(PACK - 1, (2 * h, 2 * h + 1))
+        for h in range(HALVES):
+            finish(h)
+            planes(2 * h)
+            planes(2 * h + 1)
+        for q in range(QUADS):
+            nc.sync.dma_start(
+                out=out_3[0, 4 * q : 4 * q + 4, :].bitcast(I32), in_=page_scales[32 * q : 32 * q + 4, :].bitcast(I32)
+            )

@@ -36,8 +36,8 @@ def tile_list_penguin_pair_page_kernel(
     with ExitStack() as ctx:
         lists = ctx.enter_context(tc.tile_pool(name="lists", bufs=1))
         keep = ctx.enter_context(tc.tile_pool(name="keep", bufs=1))
-        ring = ctx.enter_context(tc.tile_pool(name="ring", bufs=3))
-        psum = ctx.enter_context(tc.psum_pool(name="psum", bufs=2))
+        ring = ctx.enter_context(tc.tile_pool(name="ring", bufs=4))
+        psum = ctx.enter_context(tc.psum_pool(name="psum", bufs=4))
 
         idx = lists.tile([P, S // 16], U16, name="idx")
         idx2 = lists.tile([P, S // 16], U16, name="idx2")
@@ -46,8 +46,8 @@ def tile_list_penguin_pair_page_kernel(
         def kept(shape, dtype, name):
             return keep.tile(shape, dtype, name=name, tag=name, align_bytes=64)
 
-        v_words = [[kept([P, HALF], U32, f"vw{a}{h}") for h in range(HALVES)] for a in range(PASSES)]
-        v_rows = kept([P, S], U8, "v_rows")
+        ts = kept([P, PASSES, T], U8, "ts")
+        w2s_raw = kept([P, PASSES, H], U8, "w2sraw")
         v_scales = [kept([P, S], U8, f"vs{a}") for a in range(PASSES)]
         w1_codes = [kept([P, H], U32, f"w1c{a}") for a in range(PASSES)]
         w1_scales = [kept([P, H], U8, f"w1s{a}") for a in range(PASSES)]
@@ -59,94 +59,79 @@ def tile_list_penguin_pair_page_kernel(
         w4_codes = kept([P, N], I32, "w4c")
         w4_sc = kept([P, N], U8, "w4s")
         tare_t = kept([P, PACK], F32, "tare_t")
-        pages = [kept([P, T2], F32, f"page{t}") for t in range(PACK)]
-        sea = [[kept([P, HALF], F32, f"sea{t}{h}") for h in range(HALVES)] for t in range(PACK)]
-        wg = [[kept([P, HALF], F32, f"wg{t}{h}") for h in range(HALVES)] for t in range(PACK)]
-        hf = [kept([P, PACK, HALF], F32, f"hf{h}") for h in range(HALVES)]
+        pages = [kept([P, T2], F32, f"page{t}") for t in range(PACK - 1)]
+        units = [(0, 0, HALF), (0, HALF, S)] + [(t, 0, S) for t in range(1, PACK)]
+        sea = [kept([P, j1 - j0], F32, f"sea{n}") for n, (t, j0, j1) in enumerate(units)]
+        wg = [kept([P, j1 - j0], F32, f"wg{n}") for n, (t, j0, j1) in enumerate(units)]
+        hf = kept([P, PACK, S], F32, "hf")
 
         season_v = season.rearrange("(p t) j -> t p j", t=PACK)
         wgs_v = wgs.rearrange("(m t) j -> t m j", t=PACK)
         page_v = page0.rearrange("(p t) m -> t p m", t=PACK)
         out1_v = out_1.rearrange("(p t) m -> t p m", t=PACK)
 
-        def load_season(t, h):
-            nc.sync.dma_start(out=sea[t][h][:], in_=season_v[t][:, h * HALF : (h + 1) * HALF])
+        def load_season(n):
+            t, j0, j1 = units[n]
+            nc.sync.dma_start(out=sea[n][:], in_=season_v[t][:, j0:j1])
 
-        def load_wgs(t, h):
+        def load_wgs(n):
+            t, j0, j1 = units[n]
             for q in (0, 2, 1, 3):
-                nc.sync.dma_start(out=wg[t][h][32 * q : 32 * q + 32, :], in_=wgs_v[t][:, h * HALF : (h + 1) * HALF])
+                nc.sync.dma_start(out=wg[n][32 * q : 32 * q + 32, :], in_=wgs_v[t][:, j0:j1])
 
         def load_page(t):
             nc.sync.dma_start(out=pages[t][:], in_=page_v[t])
 
         with tc.tile_pool(name="head", bufs=1) as head:
             tw = [head.tile([P, T], I32, name=f"tw{a}", align_bytes=64) for a in range(PASSES)]
-            ts = head.tile([P, T], U8, name="ts", align_bytes=64)
             w1_raw = [head.tile([P, PACK, H], F32, name=f"w1raw{a}", align_bytes=64) for a in range(PASSES)]
             w1_bf = [head.tile([P, H, PACK], BF16, name=f"w1bf{a}", align_bytes=64) for a in range(PASSES)]
             w2_raw = head.tile([P, PASSES, 2 * H], U8, name="w2raw", align_bytes=64)
-            w2s_raw = head.tile([P, PASSES, H], U8, name="w2sraw", align_bytes=64)
 
+            nc.vector.memset(ts[:].rearrange("p a t -> p (a t)").bitcast(I32), 0)
             nc.vector.memset(w2s_raw[:].rearrange("p a c -> p (a c)").bitcast(I32), 0)
-            nc.vector.memset(ts[32:64, :].bitcast(I32), 0)
-            nc.vector.memset(ts[64:128, :].bitcast(I32), 0)
-            for a in range(PASSES):
-                nc.vector.memset(v_scales[a][:].bitcast(I32), 0)
             nc.vector.memset(w4_sc[:].bitcast(I32), 0)
 
             w1_v = w1.rearrange("(a p i) c -> a p i c", a=PASSES, i=PACK)
             tw_v = tab_words.rearrange("a p t i -> a p (t i)")
             nc.sync.dma_start(idx[:], offs)
-            nc.sync.dma_start(
-                out=ts[0:32, :].bitcast(I32), in_=tab_scales.rearrange("a q t -> (a q) t").bitcast(I32)
-            )
-            nc.sync.dma_start(out=w1_raw[0][:], in_=w1_v[0])
             nc.sync.dma_start(out=w2_raw[:].bitcast(I32), in_=w2_words.rearrange("a p c -> p a c").bitcast(I32))
-            nc.sync.dma_start(out=w1_raw[1][:], in_=w1_v[1])
+            for a in range(PASSES):
+                nc.sync.dma_start(out=w1_raw[a][:], in_=w1_v[a])
             for a in range(PASSES):
                 nc.sync.dma_start(out=tw[a][:], in_=tw_v[a].bitcast(I32))
-            for q in range(QUADS):
-                nc.gpsimd.dma_start(
-                    out=w2s_raw[32 * q : 32 * q + 4, :, :].bitcast(I32),
-                    in_=w2_scales[:, 4 * q : 4 * q + 4, :].rearrange("a r c -> r a c").bitcast(I32),
-                )
+            for planes_in, tile_in in ((tab_scales, ts), (w2_scales, w2s_raw)):
+                for q in range(QUADS):
+                    nc.gpsimd.dma_start(
+                        out=tile_in[32 * q : 32 * q + 4, :, :].bitcast(I32),
+                        in_=planes_in[:, 4 * q : 4 * q + 4, :].rearrange("a r c -> r a c").bitcast(I32),
+                    )
 
-            load_season(0, 0)
+            load_season(0)
             nc.sync.dma_start(idx2[:], offs2)
-            load_season(0, 1)
-            load_wgs(0, 0)
+            load_wgs(0)
             load_page(0)
-            load_wgs(0, 1)
+            load_season(1)
+            load_wgs(1)
+            load_season(2)
             nc.sync.dma_start(idx3[:], offs3)
             nc.sync.dma_start(out=w3_raw[:], in_=w3.rearrange("(p i) c -> p i c", i=PACK))
             nc.sync.dma_start(out=tare_t[:], in_=tare.rearrange("(p t) -> p t", t=PACK))
-            load_season(1, 0)
-            load_season(1, 1)
-            load_wgs(1, 0)
+            load_wgs(2)
             load_page(1)
-            load_wgs(1, 1)
-            for t in (2, 3):
-                for h in range(HALVES):
-                    load_season(t, h)
+            load_season(3)
+            load_season(4)
             nc.sync.dma_start(out=w4_codes[:], in_=w4_words.rearrange("a p c i -> p (a c i)").bitcast(I32))
-            for t in (2, 3):
-                load_wgs(t, 0)
-                load_page(t)
-                load_wgs(t, 1)
-
-            nc.vector.tensor_copy(v_rows[:], ts[:].indirect(idx[:]))
-            for a in range(PASSES):
-                for q in range(QUADS):
-                    first = 16 * a + 4 * q
-                    nc.gpsimd.dma_start(
-                        out=v_scales[a][32 * q : 32 * q + 4, :].bitcast(I32),
-                        in_=v_rows[first : first + 4, :].bitcast(I32),
-                    )
             for q in range(QUADS):
-                nc.gpsimd.dma_start(
+                nc.sync.dma_start(
                     out=w4_sc[32 * q : 32 * q + 4, :].bitcast(I32), in_=w4_scales[0, 4 * q : 4 * q + 4, :].bitcast(I32)
                 )
+            load_wgs(3)
+            load_page(2)
+            load_wgs(4)
 
+            for a in range(PASSES):
+                nc.vector.tensor_copy(v_scales[a][:], ts[:, a, :].indirect(idx[:]))
             for a in range(PASSES):
                 nc.vector.tensor_copy(
                     out=w2_codes[:, a, :].rearrange("p (t m b) -> p t m b", t=PACK, b=2),
@@ -165,10 +150,14 @@ def tile_list_penguin_pair_page_kernel(
                     out=w1_codes[a][:].bitcast(FP8X4), scales=w1_scales[a][:],
                     in_=w1_bf[a][:].rearrange("p c i -> p (c i)"),
                 )
+            v_words = [
+                keep.tile([P, S], U32, name=f"vw{a}", tag=("ts", "w2sraw")[a], align_bytes=64) for a in range(PASSES)
+            ]
             for a in range(PASSES):
                 for h in range(HALVES):
                     nc.vector.tensor_copy(
-                        v_words[a][h][:], tw[a][:].bitcast(U32).indirect(idx[:, h * LCOL : (h + 1) * LCOL])
+                        v_words[a][:, h * HALF : (h + 1) * HALF],
+                        tw[a][:].bitcast(U32).indirect(idx[:, h * LCOL : (h + 1) * LCOL]),
                     )
 
         tail = ctx.enter_context(tc.tile_pool(name="tail", bufs=1))
@@ -184,7 +173,7 @@ def tile_list_penguin_pair_page_kernel(
         ys = [[late([P, HALF], F32, f"y{h}{n}") for n in range(NT)] for h in range(HALVES)]
 
         def prepare_w3():
-            w3_bf = keep.tile([P, N, PACK], BF16, name="w3bf", tag="wg00", align_bytes=64)
+            w3_bf = keep.tile([P, N, PACK], BF16, name="w3bf", tag="wg1", align_bytes=64)
             nc.scalar.copy(out=w3_bf[:], in_=w3_raw[:].rearrange("p i c -> p c i"))
             for c0, c1 in ((0, 256), (256, N)):
                 nc.vector.quantize_mx(
@@ -193,50 +182,55 @@ def tile_list_penguin_pair_page_kernel(
                 )
 
         def negate_tare():
-            neg = keep.tile([P, PACK], F32, name="neg_tare", tag="wg01", align_bytes=64)
+            neg = keep.tile([P, PACK], F32, name="neg_tare", tag="sea2", align_bytes=64)
             nc.vector.tensor_scalar(neg[:], tare_t[:], -1.0, None, ALU.mult)
             return neg
 
         def products(t, h):
             cols = slice(P * t, P * (t + 1))
             jc = slice(HALF * h, HALF * (h + 1))
-            b_ps = psum.tile([P, HALF], F32, name="b_ps")
-            a_ps = psum.tile([P, HALF], F32, name="a_ps", bufs=3)
+            b_ps = psum.tile([P, HALF], F32, name="b_ps", tag="acc_b")
+            a_ps = psum.tile([P, HALF], F32, name="a_ps", tag="acc_a")
             for a in range(PASSES):
                 nc.tensor.matmul_mx(
                     out=b_ps[:], lhsT=w2_codes[:, a, 2 * P * t : 2 * P * (t + 1)].bitcast(FP4X4),
-                    lhsT_scale=w2_sc[:, a, cols], rhs=v_words[a][h][:].bitcast(FP8X4), rhs_scale=v_scales[a][:, jc],
+                    lhsT_scale=w2_sc[:, a, cols], rhs=v_words[a][:, jc].bitcast(FP8X4), rhs_scale=v_scales[a][:, jc],
                     start=(a == 0), stop=(a == PASSES - 1),
                 )
             for a in range(PASSES):
                 nc.tensor.matmul_mx(
                     out=a_ps[:], lhsT=w1_codes[a][:, cols].bitcast(FP8X4), lhsT_scale=w1_scales[a][:, cols],
-                    rhs=v_words[a][h][:].bitcast(FP8X4), rhs_scale=v_scales[a][:, jc],
+                    rhs=v_words[a][:, jc].bitcast(FP8X4), rhs_scale=v_scales[a][:, jc],
                     start=(a == 0), stop=(a == PASSES - 1),
                 )
             b_sb = ring.tile([P, HALF], F32, name="b_sb")
             nc.scalar.copy(out=b_sb[:], in_=b_ps[:])
             return a_ps, b_sb
 
-        def larger(a_ps, b_sb):
-            big = ring.tile([P, HALF], F32, name="big")
-            nc.vector.tensor_tensor(big[:], a_ps[:], b_sb[:], ALU.max)
+        def unit_products(n):
+            t, j0, j1 = units[n]
+            return [products(t, h) for h in range(j0 // HALF, j1 // HALF)]
+
+        def larger(sums):
+            big = ring.tile([P, len(sums) * HALF], F32, name="big", bufs=2)
+            for i, (a_ps, b_sb) in enumerate(sums):
+                nc.vector.tensor_tensor(big[:, i * HALF : (i + 1) * HALF], a_ps[:], b_sb[:], ALU.max)
             return big
 
-        def seasoned(t, h, big):
-            nc.vector.tensor_tensor(hf[h][:, t, :], big[:], sea[t][h][:], ALU.mult)
+        def seasoned(n, big):
+            t, j0, j1 = units[n]
+            nc.vector.tensor_tensor(hf[:, t, j0:j1], big[:], sea[n][:], ALU.mult)
 
-        def place(t, h):
-            nc.vector.tensor_tensor(
-                pages[t][:].indirect(idx2[:, h * LCOL : (h + 1) * LCOL]), hf[h][:, t, :], wg[t][h][:], ALU.mult
-            )
+        def place(n):
+            t, j0, j1 = units[n]
+            nc.vector.tensor_tensor(pages[t][:].indirect(idx2[:, j0 // 16 : j1 // 16]), hf[:, t, j0:j1], wg[n][:], ALU.mult)
 
         def round_page(t, chunks):
             for c in chunks:
                 nc.scalar.copy(out=page_pairs[c][:, t // 2, :, t % 2], in_=pages[t][:, c * CHUNK : (c + 1) * CHUNK])
 
-        def read_page(t, neg_tare):
-            for h in range(HALVES):
+        def read_page(t, neg_tare, halves):
+            for h in halves:
                 nc.vector.tensor_copy(got[h][:, t, :], pages[t][:].indirect(idx3[:, h * LCOL : (h + 1) * LCOL]))
                 nc.scalar.activation(got[h][:, t, :], got[h][:, t, :], ACT.Abs)
                 nc.scalar.activation(
@@ -249,35 +243,36 @@ def tile_list_penguin_pair_page_kernel(
             nc.vector.quantize_mx(out=codes[:].bitcast(FP8X4), scales=scales[:], in_=grouped)
             return codes, scales
 
-        def weave(pairs):
-            woven = tail.tile([P, HALF, 2], I32, name="woven", bufs=3, align_bytes=64)
-            nc.vector.tensor_copy(
+        def weave(pairs, on_scalar):
+            word = U32 if on_scalar else I32
+            woven = tail.tile([P, HALF, 2], word, name="woven", bufs=4, align_bytes=64)
+            move = nc.scalar.copy if on_scalar else nc.vector.tensor_copy
+            move(
                 out=woven[:],
-                in_=pairs[:].rearrange("p u m e -> p (u m e)").bitcast(I32).rearrange("p (u m) -> p m u", u=2),
+                in_=pairs[:].rearrange("p u m e -> p (u m e)").bitcast(word).rearrange("p (u m) -> p m u", u=2),
             )
             return woven[:].rearrange("p m u -> p (m u)").bitcast(BF16)
 
         def round_h(h):
             h_bf = late([P, HALF, PACK], BF16, f"hbf{h}")
-            nc.scalar.copy(out=h_bf[:], in_=hf[h][:].rearrange("p t j -> p j t"))
+            nc.scalar.copy(out=h_bf[:], in_=hf[:, :, h * HALF : (h + 1) * HALF].rearrange("p t j -> p j t"))
             return h_bf
 
         def tanh_part(h, h_bf):
             codes, scales = quantise(f"hq{h}", h_bf[:].rearrange("p j t -> p (j t)"))
             for n in range(NT):
                 cols = slice(P * n, P * (n + 1))
-                f_ps = psum.tile([P, HALF], F32, name="f_ps", bufs=1)
+                f_ps = psum.tile([P, HALF], F32, name="f_ps", tag="acc_a")
                 nc.tensor.matmul_mx(
                     out=f_ps[:], lhsT=w4_codes[:, cols].bitcast(FP8X4), lhsT_scale=w4_sc[:, cols],
                     rhs=codes[:].bitcast(FP8X4), rhs_scale=scales[:], start=True, stop=True,
                 )
                 nc.scalar.activation(ys[h][n][:], f_ps[:], ACT.Tanh)
 
-        def finish(h):
-            codes, scales = quantise(f"xq{h}", weave(x_pairs[h]))
+        def finish(h, codes, scales):
             for n in range(NT):
                 cols = slice(P * n, P * (n + 1))
-                e_ps = psum.tile([P, HALF], F32, name="e_ps")
+                e_ps = psum.tile([P, HALF], F32, name="e_ps", tag="acc_b")
                 nc.tensor.matmul_mx(
                     out=e_ps[:], lhsT=w3_codes[:, cols].bitcast(FP8X4), lhsT_scale=w3_scales[:, cols],
                     rhs=codes[:].bitcast(FP8X4), rhs_scale=scales[:], start=True, stop=True,
@@ -285,53 +280,61 @@ def tile_list_penguin_pair_page_kernel(
                 nc.vector.tensor_tensor(ys[h][n][:], e_ps[:], ys[h][n][:], ALU.subtract)
                 nc.sync.dma_start(out=out_0[cols, HALF * h : HALF * (h + 1)], in_=ys[h][n][:])
 
-        def planes(c):
+        def planes(c, woven):
             cols = slice(c * CHUNK, (c + 1) * CHUNK)
             nc.vector.quantize_mx(
-                out=page_codes[c][:].bitcast(FP8X4), scales=page_scales[:, cols], in_=weave(page_pairs[c])
+                out=page_codes[c][:].bitcast(FP8X4), scales=page_scales[:, cols], in_=woven
             )
             nc.sync.dma_start(
                 out=out_2.rearrange("g p m t -> p (g m t)").bitcast(I32)[:, cols], in_=page_codes[c][:].bitcast(I32)
             )
 
-        units = [(t, h) for t in range(PACK) for h in range(HALVES)]
-        sums = {}
-        bigs = {}
-        h_bfs = []
+        def page_out(t):
+            nc.sync.dma_start(out=out1_v[t], in_=pages[t][:])
+            round_page(t, range(CHUNKS))
 
-        def step(n):
-            if n + 2 < len(units):
-                sums[n + 2] = products(*units[n + 2])
-            if n + 1 < len(units):
-                bigs[n + 1] = larger(*sums[n + 1])
-            if 0 <= n < len(units):
-                seasoned(*units[n], bigs[n])
-                if units[n][0] == PACK - 1:
-                    h_bfs.append(round_h(units[n][1]))
-
-        sums[0] = products(*units[0])
-        step(-1)
-        step(0)
-        step(1)
-        for n, (t, h) in enumerate(units):
-            place(t, h)
-            step(n + 2)
-            if n == 0:
-                prepare_w3()
-            if n == 1:
-                neg_tare = negate_tare()
-            if h == HALVES - 1:
-                nc.sync.dma_start(out=out1_v[t], in_=pages[t][:])
-                read_page(t, neg_tare)
-                if t < PACK - 1:
-                    round_page(t, range(CHUNKS))
-        for h in range(HALVES):
-            tanh_part(h, h_bfs[h])
-            round_page(PACK - 1, (2 * h, 2 * h + 1))
-        for h in range(HALVES):
-            finish(h)
-            planes(2 * h)
-            planes(2 * h + 1)
+        sums = [unit_products(n) for n in range(3)]
+        seasoned(0, larger(sums[0]))
+        place(0)
+        seasoned(1, larger(sums[1]))
+        big = larger(sums[2])
+        sums.append(unit_products(3))
+        place(1)
+        seasoned(2, big)
+        neg_tare = negate_tare()
+        prepare_w3()
+        for t in range(PACK - 2):
+            big = larger(sums[t + 3])
+            if t + 4 < len(units):
+                sums.append(unit_products(t + 4))
+            page_out(t)
+            read_page(t, neg_tare, range(HALVES))
+            seasoned(t + 3, big)
+            if t + 4 == len(units):
+                h_bfs = [round_h(h) for h in range(HALVES)]
+                pages.append(keep.tile([P, T2], F32, name="page3", tag=f"sea{t + 3}", align_bytes=64))
+                load_page(PACK - 1)
+            place(t + 2)
+        tanh_part(0, h_bfs[0])
+        page_out(PACK - 2)
+        read_page(PACK - 2, neg_tare, range(HALVES))
+        tanh_part(1, h_bfs[1])
+        place(len(units) - 1)
+        nc.sync.dma_start(out=out1_v[PACK - 1], in_=pages[PACK - 1][:])
+        last = PACK - 1
+        round_page(last, (0,))
+        read_page(last, neg_tare, range(HALVES))
+        planes(0, weave(page_pairs[0], False))
+        xq = [quantise(f"xq{h}", weave(x_pairs[h], False)) for h in range(HALVES)]
+        round_page(last, (1, 2))
+        woven2 = weave(page_pairs[2], True)
+        round_page(last, (3,))
+        woven3 = weave(page_pairs[3], True)
+        finish(0, *xq[0])
+        planes(1, weave(page_pairs[1], False))
+        planes(2, woven2)
+        finish(1, *xq[1])
+        planes(3, woven3)
         for q in range(QUADS):
             nc.sync.dma_start(
                 out=out_3[0, 4 * q : 4 * q + 4, :].bitcast(I32), in_=page_scales[32 * q : 32 * q + 4, :].bitcast(I32)

@@ -46,8 +46,8 @@ def tile_list_penguin_pair_page_kernel(
         def kept(shape, dtype, name):
             return keep.tile(shape, dtype, name=name, tag=name, align_bytes=64)
 
-        ts = kept([P, PASSES, T], U8, "ts")
-        w2s_raw = kept([P, PASSES, H], U8, "w2sraw")
+        v_words = [kept([P, S], U32, f"vw{a}") for a in range(PASSES)]
+        v_rows = kept([P, S], U8, "v_rows")
         v_scales = [kept([P, S], U8, f"vs{a}") for a in range(PASSES)]
         w1_codes = [kept([P, H], U32, f"w1c{a}") for a in range(PASSES)]
         w1_scales = [kept([P, H], U8, f"w1s{a}") for a in range(PASSES)]
@@ -59,20 +59,21 @@ def tile_list_penguin_pair_page_kernel(
         w4_codes = kept([P, N], I32, "w4c")
         w4_sc = kept([P, N], U8, "w4s")
         tare_t = kept([P, PACK], F32, "tare_t")
-        pages = [kept([P, T2], F32, f"page{t}") for t in range(PACK - 1)]
-        units = [(0, 0, HALF), (0, HALF, S)] + [(t, 0, S) for t in range(1, PACK)]
-        sea = [kept([P, j1 - j0], F32, f"sea{n}") for n, (t, j0, j1) in enumerate(units)]
+        pages = [kept([P, T2], F32, f"page{t}") for t in range(PACK)]
+        made = [(0, 1, 0, HALF), (0, 1, HALF, S), (1, 2, 0, S), (2, 4, 0, S)]
+        units = [(0, 0, HALF), (0, HALF, S), (1, 0, S), (2, 0, S), (3, 0, S)]
+        sea = [kept([P, t1 - t0, j1 - j0], F32, f"sea{n}") for n, (t0, t1, j0, j1) in enumerate(made)]
         wg = [kept([P, j1 - j0], F32, f"wg{n}") for n, (t, j0, j1) in enumerate(units)]
         hf = kept([P, PACK, S], F32, "hf")
 
-        season_v = season.rearrange("(p t) j -> t p j", t=PACK)
+        season_v = season.rearrange("(p t) j -> p t j", t=PACK)
         wgs_v = wgs.rearrange("(m t) j -> t m j", t=PACK)
         page_v = page0.rearrange("(p t) m -> t p m", t=PACK)
         out1_v = out_1.rearrange("(p t) m -> t p m", t=PACK)
 
         def load_season(n):
-            t, j0, j1 = units[n]
-            nc.sync.dma_start(out=sea[n][:], in_=season_v[t][:, j0:j1])
+            t0, t1, j0, j1 = made[n]
+            nc.sync.dma_start(out=sea[n][:], in_=season_v[:, t0:t1, j0:j1])
 
         def load_wgs(n):
             t, j0, j1 = units[n]
@@ -86,26 +87,33 @@ def tile_list_penguin_pair_page_kernel(
             tw = [head.tile([P, T], I32, name=f"tw{a}", align_bytes=64) for a in range(PASSES)]
             w1_raw = [head.tile([P, PACK, H], F32, name=f"w1raw{a}", align_bytes=64) for a in range(PASSES)]
             w1_bf = [head.tile([P, H, PACK], BF16, name=f"w1bf{a}", align_bytes=64) for a in range(PASSES)]
+            ts = head.tile([P, T], U8, name="ts", align_bytes=64)
+            w2s_raw = head.tile([P, PASSES, H], U8, name="w2sraw", align_bytes=64)
             w2_raw = head.tile([P, PASSES, 2 * H], U8, name="w2raw", align_bytes=64)
 
-            nc.vector.memset(ts[:].rearrange("p a t -> p (a t)").bitcast(I32), 0)
             nc.vector.memset(w2s_raw[:].rearrange("p a c -> p (a c)").bitcast(I32), 0)
+            nc.vector.memset(ts[32:64, :].bitcast(I32), 0)
+            nc.vector.memset(ts[64:128, :].bitcast(I32), 0)
+            for a in range(PASSES):
+                nc.vector.memset(v_scales[a][:].bitcast(I32), 0)
             nc.vector.memset(w4_sc[:].bitcast(I32), 0)
 
             w1_v = w1.rearrange("(a p i) c -> a p i c", a=PASSES, i=PACK)
             tw_v = tab_words.rearrange("a p t i -> a p (t i)")
             nc.sync.dma_start(idx[:], offs)
+            nc.sync.dma_start(
+                out=ts[0:32, :].bitcast(I32), in_=tab_scales.rearrange("a q t -> (a q) t").bitcast(I32)
+            )
             nc.sync.dma_start(out=w2_raw[:].bitcast(I32), in_=w2_words.rearrange("a p c -> p a c").bitcast(I32))
             for a in range(PASSES):
                 nc.sync.dma_start(out=w1_raw[a][:], in_=w1_v[a])
             for a in range(PASSES):
                 nc.sync.dma_start(out=tw[a][:], in_=tw_v[a].bitcast(I32))
-            for planes_in, tile_in in ((tab_scales, ts), (w2_scales, w2s_raw)):
-                for q in range(QUADS):
-                    nc.gpsimd.dma_start(
-                        out=tile_in[32 * q : 32 * q + 4, :, :].bitcast(I32),
-                        in_=planes_in[:, 4 * q : 4 * q + 4, :].rearrange("a r c -> r a c").bitcast(I32),
-                    )
+            for q in range(QUADS):
+                nc.gpsimd.dma_start(
+                    out=w2s_raw[32 * q : 32 * q + 4, :, :].bitcast(I32),
+                    in_=w2_scales[:, 4 * q : 4 * q + 4, :].rearrange("a r c -> r a c").bitcast(I32),
+                )
 
             load_season(0)
             nc.sync.dma_start(idx2[:], offs2)
@@ -120,7 +128,6 @@ def tile_list_penguin_pair_page_kernel(
             load_wgs(2)
             load_page(1)
             load_season(3)
-            load_season(4)
             nc.sync.dma_start(out=w4_codes[:], in_=w4_words.rearrange("a p c i -> p (a c i)").bitcast(I32))
             for q in range(QUADS):
                 nc.sync.dma_start(
@@ -129,9 +136,16 @@ def tile_list_penguin_pair_page_kernel(
             load_wgs(3)
             load_page(2)
             load_wgs(4)
+            load_page(3)
 
+            nc.vector.tensor_copy(v_rows[:], ts[:].indirect(idx[:]))
             for a in range(PASSES):
-                nc.vector.tensor_copy(v_scales[a][:], ts[:, a, :].indirect(idx[:]))
+                for q in range(QUADS):
+                    first = 16 * a + 4 * q
+                    nc.gpsimd.dma_start(
+                        out=v_scales[a][32 * q : 32 * q + 4, :].bitcast(I32),
+                        in_=v_rows[first : first + 4, :].bitcast(I32),
+                    )
             for a in range(PASSES):
                 nc.vector.tensor_copy(
                     out=w2_codes[:, a, :].rearrange("p (t m b) -> p t m b", t=PACK, b=2),
@@ -150,9 +164,6 @@ def tile_list_penguin_pair_page_kernel(
                     out=w1_codes[a][:].bitcast(FP8X4), scales=w1_scales[a][:],
                     in_=w1_bf[a][:].rearrange("p c i -> p (c i)"),
                 )
-            v_words = [
-                keep.tile([P, S], U32, name=f"vw{a}", tag=("ts", "w2sraw")[a], align_bytes=64) for a in range(PASSES)
-            ]
             for a in range(PASSES):
                 for h in range(HALVES):
                     nc.vector.tensor_copy(
@@ -163,12 +174,11 @@ def tile_list_penguin_pair_page_kernel(
         tail = ctx.enter_context(tc.tile_pool(name="tail", bufs=1))
 
         def late(shape, dtype, name):
-            return tail.tile(shape, dtype, name=name, align_bytes=64)
+            return tail.tile(shape, dtype, name=name, tag=name, align_bytes=64)
 
         page_pairs = [late([P, 2, CHUNK, 2], BF16, f"pp{c}") for c in range(CHUNKS)]
         page_codes = [late([P, CHUNK], U32, f"pc{c}") for c in range(CHUNKS)]
         page_scales = late([P, T2], U8, "ps")
-        got = [late([P, PACK, HALF], F32, f"got{h}") for h in range(HALVES)]
         x_pairs = [late([P, 2, HALF, 2], BF16, f"xp{h}") for h in range(HALVES)]
         ys = [[late([P, HALF], F32, f"y{h}{n}") for n in range(NT)] for h in range(HALVES)]
 
@@ -186,30 +196,35 @@ def tile_list_penguin_pair_page_kernel(
             nc.vector.tensor_scalar(neg[:], tare_t[:], -1.0, None, ALU.mult)
             return neg
 
-        def products(t, h):
+        def product_pass(t, h, a, banks):
             cols = slice(P * t, P * (t + 1))
             jc = slice(HALF * h, HALF * (h + 1))
-            b_ps = psum.tile([P, HALF], F32, name="b_ps", tag="acc_b")
-            a_ps = psum.tile([P, HALF], F32, name="a_ps", tag="acc_a")
-            for a in range(PASSES):
-                nc.tensor.matmul_mx(
-                    out=b_ps[:], lhsT=w2_codes[:, a, 2 * P * t : 2 * P * (t + 1)].bitcast(FP4X4),
-                    lhsT_scale=w2_sc[:, a, cols], rhs=v_words[a][:, jc].bitcast(FP8X4), rhs_scale=v_scales[a][:, jc],
-                    start=(a == 0), stop=(a == PASSES - 1),
-                )
-            for a in range(PASSES):
-                nc.tensor.matmul_mx(
-                    out=a_ps[:], lhsT=w1_codes[a][:, cols].bitcast(FP8X4), lhsT_scale=w1_scales[a][:, cols],
-                    rhs=v_words[a][:, jc].bitcast(FP8X4), rhs_scale=v_scales[a][:, jc],
-                    start=(a == 0), stop=(a == PASSES - 1),
-                )
-            b_sb = ring.tile([P, HALF], F32, name="b_sb")
-            nc.scalar.copy(out=b_sb[:], in_=b_ps[:])
-            return a_ps, b_sb
+            moving = dict(
+                rhs=v_words[a][:, jc].bitcast(FP8X4), rhs_scale=v_scales[a][:, jc],
+                start=(a == 0), stop=(a == PASSES - 1),
+            )
+            nc.tensor.matmul_mx(
+                out=banks[1][:], lhsT=w2_codes[:, a, 2 * P * t : 2 * P * (t + 1)].bitcast(FP4X4),
+                lhsT_scale=w2_sc[:, a, cols], **moving,
+            )
+            nc.tensor.matmul_mx(
+                out=banks[0][:], lhsT=w1_codes[a][:, cols].bitcast(FP8X4), lhsT_scale=w1_scales[a][:, cols], **moving
+            )
 
-        def unit_products(n):
-            t, j0, j1 = units[n]
-            return [products(t, h) for h in range(j0 // HALF, j1 // HALF)]
+        def products(groups):
+            banks = [
+                (psum.tile([P, HALF], F32, name="a_ps", tag="acc_a"), psum.tile([P, HALF], F32, name="b_ps", tag="acc_b"))
+                for group in groups
+            ]
+            for (t, h), pair in zip(groups, banks):
+                product_pass(t, h, 0, pair)
+            sums = []
+            for (t, h), pair in zip(groups, banks):
+                product_pass(t, h, 1, pair)
+                b_sb = ring.tile([P, HALF], F32, name="b_sb")
+                nc.scalar.copy(out=b_sb[:], in_=pair[1][:])
+                sums.append((pair[0], b_sb))
+            return sums
 
         def larger(sums):
             big = ring.tile([P, len(sums) * HALF], F32, name="big", bufs=2)
@@ -218,8 +233,10 @@ def tile_list_penguin_pair_page_kernel(
             return big
 
         def seasoned(n, big):
-            t, j0, j1 = units[n]
-            nc.vector.tensor_tensor(hf[:, t, j0:j1], big[:], sea[n][:], ALU.mult)
+            t0, t1, j0, j1 = made[n]
+            nc.vector.tensor_tensor(
+                hf[:, t0:t1, j0:j1], big[:].rearrange("p (t j) -> p t j", t=t1 - t0), sea[n][:], ALU.mult
+            )
 
         def place(n):
             t, j0, j1 = units[n]
@@ -229,12 +246,15 @@ def tile_list_penguin_pair_page_kernel(
             for c in chunks:
                 nc.scalar.copy(out=page_pairs[c][:, t // 2, :, t % 2], in_=pages[t][:, c * CHUNK : (c + 1) * CHUNK])
 
-        def read_page(t, neg_tare, halves):
-            for h in halves:
-                nc.vector.tensor_copy(got[h][:, t, :], pages[t][:].indirect(idx3[:, h * LCOL : (h + 1) * LCOL]))
-                nc.scalar.activation(got[h][:, t, :], got[h][:, t, :], ACT.Abs)
+        def read_page(t, halves, neg_tare):
+            got = tail.tile([P, len(halves) * HALF], F32, name="got", bufs=3, align_bytes=64)
+            entries = idx3[:, halves[0] * LCOL : (halves[-1] + 1) * LCOL]
+            nc.vector.tensor_copy(got[:], pages[t][:].indirect(entries))
+            nc.scalar.activation(got[:], got[:], ACT.Abs)
+            for i, h in enumerate(halves):
                 nc.scalar.activation(
-                    x_pairs[h][:, t // 2, :, t % 2], got[h][:, t, :], ACT.Identity, bias=neg_tare[:, t : t + 1]
+                    x_pairs[h][:, t // 2, :, t % 2], got[:, i * HALF : (i + 1) * HALF], ACT.Identity,
+                    bias=neg_tare[:, t : t + 1],
                 )
 
         def quantise(name, grouped):
@@ -293,37 +313,37 @@ def tile_list_penguin_pair_page_kernel(
             nc.sync.dma_start(out=out1_v[t], in_=pages[t][:])
             round_page(t, range(CHUNKS))
 
-        sums = [unit_products(n) for n in range(3)]
-        seasoned(0, larger(sums[0]))
+        sums = products([(t, h) for t in (0, 1) for h in range(HALVES)])
+        seasoned(0, larger(sums[0:1]))
         place(0)
-        seasoned(1, larger(sums[1]))
-        big = larger(sums[2])
-        sums.append(unit_products(3))
+        big1 = larger(sums[1:2])
+        big2 = larger(sums[2:4])
+        seasoned(1, big1)
+        last_sums = [pair for t in (2, 3) for h in range(HALVES) for pair in products([(t, h)])]
+        seasoned(2, big2)
         place(1)
-        seasoned(2, big)
         neg_tare = negate_tare()
         prepare_w3()
-        for t in range(PACK - 2):
-            big = larger(sums[t + 3])
-            if t + 4 < len(units):
-                sums.append(unit_products(t + 4))
-            page_out(t)
-            read_page(t, neg_tare, range(HALVES))
-            seasoned(t + 3, big)
-            if t + 4 == len(units):
-                h_bfs = [round_h(h) for h in range(HALVES)]
-                pages.append(keep.tile([P, T2], F32, name="page3", tag=f"sea{t + 3}", align_bytes=64))
-                load_page(PACK - 1)
-            place(t + 2)
-        tanh_part(0, h_bfs[0])
-        page_out(PACK - 2)
-        read_page(PACK - 2, neg_tare, range(HALVES))
-        tanh_part(1, h_bfs[1])
-        place(len(units) - 1)
-        nc.sync.dma_start(out=out1_v[PACK - 1], in_=pages[PACK - 1][:])
+        place(2)
+        page_out(0)
+        read_page(0, (0, 1), neg_tare)
+        big3 = larger(last_sums)
+        page_out(1)
+        read_page(1, (0,), neg_tare)
+        seasoned(3, big3)
+        h_bfs = [round_h(h) for h in range(HALVES)]
+        read_page(1, (1,), neg_tare)
+        place(3)
+        place(4)
+        page_out(2)
+        read_page(2, (0, 1), neg_tare)
         last = PACK - 1
+        nc.sync.dma_start(out=out1_v[last], in_=pages[last][:])
         round_page(last, (0,))
-        read_page(last, neg_tare, range(HALVES))
+        read_page(last, (0,), neg_tare)
+        tanh_part(0, h_bfs[0])
+        read_page(last, (1,), neg_tare)
+        tanh_part(1, h_bfs[1])
         planes(0, weave(page_pairs[0], False))
         xq = [quantise(f"xq{h}", weave(x_pairs[h], False)) for h in range(HALVES)]
         round_page(last, (1, 2))

@@ -21,11 +21,19 @@ PACK = 4
 PASSES = K // (P * PACK)
 HALF = 512
 HALVES = S // HALF
-LCOL = HALF // 16
+PER_COL = 16
 QUADS = 4
+QUAD = P // QUADS
+ROWS = 4
 CHUNK = 512
 CHUNKS = T2 // CHUNK
 NT = N // P
+HELD_BANKS = 6
+PASSING_BANKS = 2
+W3_CUTS = ((0, 256), (256, N))
+
+MADE = ((0, 1, 0, HALF), (0, 1, HALF, S), (1, 2, 0, S), (2, 4, 0, S))
+PLACED = ((0, 0, HALF), (0, HALF, S), (1, 0, S), (2, 0, S), (3, 0, S))
 
 
 def tile_list_penguin_pair_page_kernel(
@@ -36,34 +44,35 @@ def tile_list_penguin_pair_page_kernel(
     with ExitStack() as ctx:
         lists = ctx.enter_context(tc.tile_pool(name="lists", bufs=1))
         keep = ctx.enter_context(tc.tile_pool(name="keep", bufs=1))
-        ring = ctx.enter_context(tc.tile_pool(name="ring", bufs=4))
-        psum = ctx.enter_context(tc.psum_pool(name="psum", bufs=4))
+        ring = ctx.enter_context(tc.tile_pool(name="ring", bufs=PACK * HALVES))
+        psum = ctx.enter_context(tc.psum_pool(name="psum", bufs=1))
 
-        idx = lists.tile([P, S // 16], U16, name="idx")
-        idx2 = lists.tile([P, S // 16], U16, name="idx2")
-        idx3 = lists.tile([P, S // 16], U16, name="idx3")
+        idx = lists.tile([P, S // PER_COL], U16, name="idx")
+        idx2 = lists.tile([P, S // PER_COL], U16, name="idx2")
+        idx3 = lists.tile([P, S // PER_COL], U16, name="idx3")
 
-        def kept(shape, dtype, name):
-            return keep.tile(shape, dtype, name=name, tag=name, align_bytes=64)
+        def kept(shape, dtype, name, slot=None):
+            return keep.tile(shape, dtype, name=name, tag=slot or name, align_bytes=64)
+
+        def entries(list_tile, j0, j1):
+            return list_tile[:, j0 // PER_COL : j1 // PER_COL]
 
         v_words = [kept([P, S], U32, f"vw{a}") for a in range(PASSES)]
         v_rows = kept([P, S], U8, "v_rows")
-        v_scales = [kept([P, S], U8, f"vs{a}") for a in range(PASSES)]
+        v_scales = kept([P, PASSES, S], U8, "v_scales")
         w1_codes = [kept([P, H], U32, f"w1c{a}") for a in range(PASSES)]
         w1_scales = [kept([P, H], U8, f"w1s{a}") for a in range(PASSES)]
         w2_codes = kept([P, PASSES, 2 * H], U8, "w2c")
-        w2_sc = kept([P, PASSES, H], U8, "w2s")
+        w2_planes = kept([P, PASSES, H], U8, "w2s")
         w3_raw = kept([P, PACK, N], F32, "w3raw")
         w3_codes = kept([P, N], U32, "w3c")
         w3_scales = kept([P, N], U8, "w3s")
         w4_codes = kept([P, N], I32, "w4c")
-        w4_sc = kept([P, N], U8, "w4s")
+        w4_planes = kept([P, N], U8, "w4s")
         tare_t = kept([P, PACK], F32, "tare_t")
         pages = [kept([P, T2], F32, f"page{t}") for t in range(PACK)]
-        made = [(0, 1, 0, HALF), (0, 1, HALF, S), (1, 2, 0, S), (2, 4, 0, S)]
-        units = [(0, 0, HALF), (0, HALF, S), (1, 0, S), (2, 0, S), (3, 0, S)]
-        sea = [kept([P, t1 - t0, j1 - j0], F32, f"sea{n}") for n, (t0, t1, j0, j1) in enumerate(made)]
-        wg = [kept([P, j1 - j0], F32, f"wg{n}") for n, (t, j0, j1) in enumerate(units)]
+        sea = [kept([P, t1 - t0, j1 - j0], F32, f"sea{n}") for n, (t0, t1, j0, j1) in enumerate(MADE)]
+        wg = [kept([P, j1 - j0], F32, f"wg{n}") for n, (t, j0, j1) in enumerate(PLACED)]
         hf = kept([P, PACK, S], F32, "hf")
 
         season_v = season.rearrange("(p t) j -> p t j", t=PACK)
@@ -72,13 +81,13 @@ def tile_list_penguin_pair_page_kernel(
         out1_v = out_1.rearrange("(p t) m -> t p m", t=PACK)
 
         def load_season(n):
-            t0, t1, j0, j1 = made[n]
+            t0, t1, j0, j1 = MADE[n]
             nc.sync.dma_start(out=sea[n][:], in_=season_v[:, t0:t1, j0:j1])
 
         def load_wgs(n):
-            t, j0, j1 = units[n]
+            t, j0, j1 = PLACED[n]
             for q in (0, 2, 1, 3):
-                nc.sync.dma_start(out=wg[n][32 * q : 32 * q + 32, :], in_=wgs_v[t][:, j0:j1])
+                nc.sync.dma_start(out=wg[n][QUAD * q : QUAD * (q + 1), :], in_=wgs_v[t][:, j0:j1])
 
         def load_page(t):
             nc.sync.dma_start(out=pages[t][:], in_=page_v[t])
@@ -92,18 +101,15 @@ def tile_list_penguin_pair_page_kernel(
             w2_raw = head.tile([P, PASSES, 2 * H], U8, name="w2raw", align_bytes=64)
 
             nc.vector.memset(w2s_raw[:].rearrange("p a c -> p (a c)").bitcast(I32), 0)
-            nc.vector.memset(ts[32:64, :].bitcast(I32), 0)
-            nc.vector.memset(ts[64:128, :].bitcast(I32), 0)
-            for a in range(PASSES):
-                nc.vector.memset(v_scales[a][:].bitcast(I32), 0)
-            nc.vector.memset(w4_sc[:].bitcast(I32), 0)
+            nc.vector.memset(ts[QUAD : 2 * QUAD, :].bitcast(I32), 0)
+            nc.vector.memset(ts[2 * QUAD : P, :].bitcast(I32), 0)
+            nc.vector.memset(v_scales[:].rearrange("p a j -> p (a j)").bitcast(I32), 0)
+            nc.vector.memset(w4_planes[:].bitcast(I32), 0)
 
             w1_v = w1.rearrange("(a p i) c -> a p i c", a=PASSES, i=PACK)
             tw_v = tab_words.rearrange("a p t i -> a p (t i)")
             nc.sync.dma_start(idx[:], offs)
-            nc.sync.dma_start(
-                out=ts[0:32, :].bitcast(I32), in_=tab_scales.rearrange("a q t -> (a q) t").bitcast(I32)
-            )
+            nc.sync.dma_start(out=ts[0:QUAD, :].bitcast(I32), in_=tab_scales.rearrange("a q t -> q a t").bitcast(I32))
             nc.sync.dma_start(out=w2_raw[:].bitcast(I32), in_=w2_words.rearrange("a p c -> p a c").bitcast(I32))
             for a in range(PASSES):
                 nc.sync.dma_start(out=w1_raw[a][:], in_=w1_v[a])
@@ -111,48 +117,47 @@ def tile_list_penguin_pair_page_kernel(
                 nc.sync.dma_start(out=tw[a][:], in_=tw_v[a].bitcast(I32))
             for q in range(QUADS):
                 nc.gpsimd.dma_start(
-                    out=w2s_raw[32 * q : 32 * q + 4, :, :].bitcast(I32),
-                    in_=w2_scales[:, 4 * q : 4 * q + 4, :].rearrange("a r c -> r a c").bitcast(I32),
+                    out=w2s_raw[QUAD * q : QUAD * q + ROWS, :, :].bitcast(I32),
+                    in_=w2_scales[:, ROWS * q : ROWS * (q + 1), :].rearrange("a r c -> r a c").bitcast(I32),
                 )
 
             load_season(0)
             nc.sync.dma_start(idx2[:], offs2)
+            load_season(1)
             load_wgs(0)
             load_page(0)
-            load_season(1)
             load_wgs(1)
-            load_season(2)
             nc.sync.dma_start(idx3[:], offs3)
-            nc.sync.dma_start(out=w3_raw[:], in_=w3.rearrange("(p i) c -> p i c", i=PACK))
             nc.sync.dma_start(out=tare_t[:], in_=tare.rearrange("(p t) -> p t", t=PACK))
+            load_season(2)
             load_wgs(2)
             load_page(1)
+            load_wgs(3)
+            load_page(2)
             load_season(3)
+            nc.sync.dma_start(out=w3_raw[:], in_=w3.rearrange("(p i) c -> p i c", i=PACK))
             nc.sync.dma_start(out=w4_codes[:], in_=w4_words.rearrange("a p c i -> p (a c i)").bitcast(I32))
             for q in range(QUADS):
                 nc.sync.dma_start(
-                    out=w4_sc[32 * q : 32 * q + 4, :].bitcast(I32), in_=w4_scales[0, 4 * q : 4 * q + 4, :].bitcast(I32)
+                    out=w4_planes[QUAD * q : QUAD * q + ROWS, :].bitcast(I32),
+                    in_=w4_scales[0, ROWS * q : ROWS * (q + 1), :].bitcast(I32),
                 )
-            load_wgs(3)
-            load_page(2)
             load_wgs(4)
             load_page(3)
 
             nc.vector.tensor_copy(v_rows[:], ts[:].indirect(idx[:]))
-            for a in range(PASSES):
-                for q in range(QUADS):
-                    first = 16 * a + 4 * q
-                    nc.gpsimd.dma_start(
-                        out=v_scales[a][32 * q : 32 * q + 4, :].bitcast(I32),
-                        in_=v_rows[first : first + 4, :].bitcast(I32),
-                    )
+            for q in range(QUADS):
+                nc.gpsimd.dma_start(
+                    out=v_scales[QUAD * q : QUAD * q + ROWS, :, :].rearrange("p a j -> p (a j)").bitcast(I32),
+                    in_=v_rows[PASSES * ROWS * q : PASSES * ROWS * (q + 1), :].bitcast(I32),
+                )
             for a in range(PASSES):
                 nc.vector.tensor_copy(
-                    out=w2_codes[:, a, :].rearrange("p (t m b) -> p t m b", t=PACK, b=2),
-                    in_=w2_raw[:, a, :].rearrange("p (m t b) -> p t m b", t=PACK, b=2),
+                    out=w2_codes[:, a, :].bitcast(U16).rearrange("p (t m) -> p t m", t=PACK),
+                    in_=w2_raw[:, a, :].bitcast(U16).rearrange("p (m t) -> p t m", t=PACK),
                 )
             nc.vector.tensor_copy(
-                out=w2_sc[:].rearrange("p a (t m) -> p a t m", t=PACK),
+                out=w2_planes[:].rearrange("p a (t m) -> p a t m", t=PACK),
                 in_=w2s_raw[:].rearrange("p a (m t) -> p a t m", t=PACK),
             )
             for a in range(PASSES):
@@ -168,7 +173,7 @@ def tile_list_penguin_pair_page_kernel(
                 for h in range(HALVES):
                     nc.vector.tensor_copy(
                         v_words[a][:, h * HALF : (h + 1) * HALF],
-                        tw[a][:].bitcast(U32).indirect(idx[:, h * LCOL : (h + 1) * LCOL]),
+                        tw[a][:].bitcast(U32).indirect(entries(idx, h * HALF, (h + 1) * HALF)),
                     )
 
         tail = ctx.enter_context(tc.tile_pool(name="tail", bufs=1))
@@ -182,17 +187,22 @@ def tile_list_penguin_pair_page_kernel(
         x_pairs = [late([P, 2, HALF, 2], BF16, f"xp{h}") for h in range(HALVES)]
         ys = [[late([P, HALF], F32, f"y{h}{n}") for n in range(NT)] for h in range(HALVES)]
 
+        def interleave(grouped, rows):
+            nc.scalar.copy(
+                out=grouped.rearrange("p (c i) t -> p c t i", i=4), in_=rows.rearrange("p t (c i) -> p c t i", i=4)
+            )
+
         def prepare_w3():
-            w3_bf = keep.tile([P, N, PACK], BF16, name="w3bf", tag="wg1", align_bytes=64)
-            nc.scalar.copy(out=w3_bf[:], in_=w3_raw[:].rearrange("p i c -> p c i"))
-            for c0, c1 in ((0, 256), (256, N)):
+            w3_bf = kept([P, N, PACK], BF16, "w3bf", slot="big1")
+            interleave(w3_bf[:], w3_raw[:])
+            for c0, c1 in W3_CUTS:
                 nc.vector.quantize_mx(
                     out=w3_codes[:, c0:c1].bitcast(FP8X4), scales=w3_scales[:, c0:c1],
                     in_=w3_bf[:, c0:c1, :].rearrange("p c i -> p (c i)"),
                 )
 
         def negate_tare():
-            neg = keep.tile([P, PACK], F32, name="neg_tare", tag="sea2", align_bytes=64)
+            neg = kept([P, PACK], F32, "neg_tare", slot="sea2")
             nc.vector.tensor_scalar(neg[:], tare_t[:], -1.0, None, ALU.mult)
             return neg
 
@@ -200,12 +210,12 @@ def tile_list_penguin_pair_page_kernel(
             cols = slice(P * t, P * (t + 1))
             jc = slice(HALF * h, HALF * (h + 1))
             moving = dict(
-                rhs=v_words[a][:, jc].bitcast(FP8X4), rhs_scale=v_scales[a][:, jc],
+                rhs=v_words[a][:, jc].bitcast(FP8X4), rhs_scale=v_scales[:, a, jc],
                 start=(a == 0), stop=(a == PASSES - 1),
             )
             nc.tensor.matmul_mx(
                 out=banks[1][:], lhsT=w2_codes[:, a, 2 * P * t : 2 * P * (t + 1)].bitcast(FP4X4),
-                lhsT_scale=w2_sc[:, a, cols], **moving,
+                lhsT_scale=w2_planes[:, a, cols], **moving,
             )
             nc.tensor.matmul_mx(
                 out=banks[0][:], lhsT=w1_codes[a][:, cols].bitcast(FP8X4), lhsT_scale=w1_scales[a][:, cols], **moving
@@ -213,7 +223,10 @@ def tile_list_penguin_pair_page_kernel(
 
         def products(groups):
             banks = [
-                (psum.tile([P, HALF], F32, name="a_ps", tag="acc_a"), psum.tile([P, HALF], F32, name="b_ps", tag="acc_b"))
+                (
+                    psum.tile([P, HALF], F32, name="a_ps", tag="held", bufs=HELD_BANKS),
+                    psum.tile([P, HALF], F32, name="b_ps", tag="passing", bufs=PASSING_BANKS),
+                )
                 for group in groups
             ]
             for (t, h), pair in zip(groups, banks):
@@ -226,21 +239,21 @@ def tile_list_penguin_pair_page_kernel(
                 sums.append((pair[0], b_sb))
             return sums
 
-        def larger(sums):
-            big = ring.tile([P, len(sums) * HALF], F32, name="big", bufs=2)
+        def larger(sums, slot):
+            big = kept([P, len(sums) * HALF], F32, "big", slot=slot)
             for i, (a_ps, b_sb) in enumerate(sums):
                 nc.vector.tensor_tensor(big[:, i * HALF : (i + 1) * HALF], a_ps[:], b_sb[:], ALU.max)
             return big
 
         def seasoned(n, big):
-            t0, t1, j0, j1 = made[n]
+            t0, t1, j0, j1 = MADE[n]
             nc.vector.tensor_tensor(
                 hf[:, t0:t1, j0:j1], big[:].rearrange("p (t j) -> p t j", t=t1 - t0), sea[n][:], ALU.mult
             )
 
         def place(n):
-            t, j0, j1 = units[n]
-            nc.vector.tensor_tensor(pages[t][:].indirect(idx2[:, j0 // 16 : j1 // 16]), hf[:, t, j0:j1], wg[n][:], ALU.mult)
+            t, j0, j1 = PLACED[n]
+            nc.vector.tensor_tensor(pages[t][:].indirect(entries(idx2, j0, j1)), hf[:, t, j0:j1], wg[n][:], ALU.mult)
 
         def round_page(t, chunks):
             for c in chunks:
@@ -248,8 +261,9 @@ def tile_list_penguin_pair_page_kernel(
 
         def read_page(t, halves, neg_tare):
             got = tail.tile([P, len(halves) * HALF], F32, name="got", bufs=3, align_bytes=64)
-            entries = idx3[:, halves[0] * LCOL : (halves[-1] + 1) * LCOL]
-            nc.vector.tensor_copy(got[:], pages[t][:].indirect(entries))
+            nc.vector.tensor_copy(
+                got[:], pages[t][:].indirect(entries(idx3, halves[0] * HALF, (halves[-1] + 1) * HALF))
+            )
             nc.scalar.activation(got[:], got[:], ACT.Abs)
             for i, h in enumerate(halves):
                 nc.scalar.activation(
@@ -264,27 +278,27 @@ def tile_list_penguin_pair_page_kernel(
             return codes, scales
 
         def weave(pairs, on_scalar):
-            word = U32 if on_scalar else I32
-            woven = tail.tile([P, HALF, 2], word, name="woven", bufs=4, align_bytes=64)
+            pair = U32 if on_scalar else I32
+            woven = tail.tile([P, HALF, 2], pair, name="woven", bufs=3, align_bytes=64)
             move = nc.scalar.copy if on_scalar else nc.vector.tensor_copy
             move(
                 out=woven[:],
-                in_=pairs[:].rearrange("p u m e -> p (u m e)").bitcast(word).rearrange("p (u m) -> p m u", u=2),
+                in_=pairs[:].rearrange("p u m e -> p (u m e)").bitcast(pair).rearrange("p (u m) -> p m u", u=2),
             )
             return woven[:].rearrange("p m u -> p (m u)").bitcast(BF16)
 
         def round_h(h):
             h_bf = late([P, HALF, PACK], BF16, f"hbf{h}")
-            nc.scalar.copy(out=h_bf[:], in_=hf[:, :, h * HALF : (h + 1) * HALF].rearrange("p t j -> p j t"))
+            interleave(h_bf[:], hf[:, :, h * HALF : (h + 1) * HALF])
             return h_bf
 
         def tanh_part(h, h_bf):
             codes, scales = quantise(f"hq{h}", h_bf[:].rearrange("p j t -> p (j t)"))
             for n in range(NT):
                 cols = slice(P * n, P * (n + 1))
-                f_ps = psum.tile([P, HALF], F32, name="f_ps", tag="acc_a")
+                f_ps = psum.tile([P, HALF], F32, name="f_ps", tag="passing", bufs=PASSING_BANKS)
                 nc.tensor.matmul_mx(
-                    out=f_ps[:], lhsT=w4_codes[:, cols].bitcast(FP8X4), lhsT_scale=w4_sc[:, cols],
+                    out=f_ps[:], lhsT=w4_codes[:, cols].bitcast(FP8X4), lhsT_scale=w4_planes[:, cols],
                     rhs=codes[:].bitcast(FP8X4), rhs_scale=scales[:], start=True, stop=True,
                 )
                 nc.scalar.activation(ys[h][n][:], f_ps[:], ACT.Tanh)
@@ -292,7 +306,7 @@ def tile_list_penguin_pair_page_kernel(
         def finish(h, codes, scales):
             for n in range(NT):
                 cols = slice(P * n, P * (n + 1))
-                e_ps = psum.tile([P, HALF], F32, name="e_ps", tag="acc_b")
+                e_ps = psum.tile([P, HALF], F32, name="e_ps", tag="held", bufs=HELD_BANKS)
                 nc.tensor.matmul_mx(
                     out=e_ps[:], lhsT=w3_codes[:, cols].bitcast(FP8X4), lhsT_scale=w3_scales[:, cols],
                     rhs=codes[:].bitcast(FP8X4), rhs_scale=scales[:], start=True, stop=True,
@@ -302,9 +316,7 @@ def tile_list_penguin_pair_page_kernel(
 
         def planes(c, woven):
             cols = slice(c * CHUNK, (c + 1) * CHUNK)
-            nc.vector.quantize_mx(
-                out=page_codes[c][:].bitcast(FP8X4), scales=page_scales[:, cols], in_=woven
-            )
+            nc.vector.quantize_mx(out=page_codes[c][:].bitcast(FP8X4), scales=page_scales[:, cols], in_=woven)
             nc.sync.dma_start(
                 out=out_2.rearrange("g p m t -> p (g m t)").bitcast(I32)[:, cols], in_=page_codes[c][:].bitcast(I32)
             )
@@ -313,37 +325,40 @@ def tile_list_penguin_pair_page_kernel(
             nc.sync.dma_start(out=out1_v[t], in_=pages[t][:])
             round_page(t, range(CHUNKS))
 
-        sums = products([(t, h) for t in (0, 1) for h in range(HALVES)])
-        seasoned(0, larger(sums[0:1]))
-        place(0)
-        big1 = larger(sums[1:2])
-        big2 = larger(sums[2:4])
+        sums = products([(0, h) for h in range(HALVES)])
+        for t in range(1, PACK):
+            for h in range(HALVES):
+                sums.extend(products([(t, h)]))
+        big0 = larger(sums[0:1], "big0")
+        big1 = larger(sums[1:2], "big1")
+        seasoned(0, big0)
         seasoned(1, big1)
-        last_sums = [pair for t in (2, 3) for h in range(HALVES) for pair in products([(t, h)])]
-        seasoned(2, big2)
+        place(0)
+        big2 = larger(sums[2:4], "wg0")
         place(1)
+        seasoned(2, big2)
         neg_tare = negate_tare()
-        prepare_w3()
-        place(2)
         page_out(0)
         read_page(0, (0, 1), neg_tare)
-        big3 = larger(last_sums)
+        place(2)
+        big3 = larger(sums[4:8], "wg1")
         page_out(1)
         read_page(1, (0,), neg_tare)
         seasoned(3, big3)
         h_bfs = [round_h(h) for h in range(HALVES)]
         read_page(1, (1,), neg_tare)
         place(3)
-        place(4)
         page_out(2)
         read_page(2, (0, 1), neg_tare)
+        for h in range(HALVES):
+            tanh_part(h, h_bfs[h])
+        prepare_w3()
+        place(4)
         last = PACK - 1
         nc.sync.dma_start(out=out1_v[last], in_=pages[last][:])
         round_page(last, (0,))
         read_page(last, (0,), neg_tare)
-        tanh_part(0, h_bfs[0])
         read_page(last, (1,), neg_tare)
-        tanh_part(1, h_bfs[1])
         planes(0, weave(page_pairs[0], False))
         xq = [quantise(f"xq{h}", weave(x_pairs[h], False)) for h in range(HALVES)]
         round_page(last, (1, 2))
@@ -357,5 +372,6 @@ def tile_list_penguin_pair_page_kernel(
         planes(3, woven3)
         for q in range(QUADS):
             nc.sync.dma_start(
-                out=out_3[0, 4 * q : 4 * q + 4, :].bitcast(I32), in_=page_scales[32 * q : 32 * q + 4, :].bitcast(I32)
+                out=out_3[0, ROWS * q : ROWS * (q + 1), :].bitcast(I32),
+                in_=page_scales[QUAD * q : QUAD * q + ROWS, :].bitcast(I32),
             )

from contextlib import ExitStack

import concourse.mybir as mybir

K, T, S, H, T2, N = 1024, 4096, 1024, 512, 2048, 384
FLOPS = 2 * (2 * K * H * S + 2 * H * N * S)

F32 = mybir.dt.float32
BF16 = mybir.dt.bfloat16
I32 = mybir.dt.int32
U32 = mybir.dt.uint32
U16 = mybir.dt.uint16
U8 = mybir.dt.uint8
FP8X4 = mybir.dt.float8_e4m3fn_x4
FP4X4 = mybir.dt.float4_e2m1fn_x4
ALU = mybir.AluOpType
ACT = mybir.ActivationFunctionType

P = 128
PACK = 4
PASSES = K // (P * PACK)
HALF = 512
HALVES = S // HALF
PER_COL = 16
QUADS = 4
QUAD = P // QUADS
ROWS = 4
CHUNK = 512
CHUNKS = T2 // CHUNK
NT = N // P
HELD_BANKS = 6
PASSING_BANKS = 2
W3_CUTS = ((0, 256), (256, N))

MADE = ((0, 1, 0, HALF), (0, 1, HALF, S), (1, 2, 0, S), (2, 4, 0, S))
PLACED = ((0, 0, HALF), (0, HALF, S), (1, 0, S), (2, 0, S), (3, 0, S))


def tile_list_penguin_pair_page_kernel(
    tc, tab_words, tab_scales, offs, offs2, offs3, w1, w2_words, w2_scales, season, wgs, page0, tare, w3,
    w4_words, w4_scales, out_0, out_1, out_2, out_3,
):
    nc = tc.nc
    with ExitStack() as ctx:
        lists = ctx.enter_context(tc.tile_pool(name="lists", bufs=1))
        keep = ctx.enter_context(tc.tile_pool(name="keep", bufs=1))
        ring = ctx.enter_context(tc.tile_pool(name="ring", bufs=PACK * HALVES))
        psum = ctx.enter_context(tc.psum_pool(name="psum", bufs=1))

        idx = lists.tile([P, S // PER_COL], U16, name="idx")
        idx2 = lists.tile([P, S // PER_COL], U16, name="idx2")
        idx3 = lists.tile([P, S // PER_COL], U16, name="idx3")

        def kept(shape, dtype, name, slot=None):
            return keep.tile(shape, dtype, name=name, tag=slot or name, align_bytes=64)

        def entries(list_tile, j0, j1):
            return list_tile[:, j0 // PER_COL : j1 // PER_COL]

        v_words = [kept([P, S], U32, f"vw{a}") for a in range(PASSES)]
        v_rows = kept([P, S], U8, "v_rows")
        v_scales = kept([P, PASSES, S], U8, "v_scales")
        w1_codes = [kept([P, H], U32, f"w1c{a}") for a in range(PASSES)]
        w1_scales = [kept([P, H], U8, f"w1s{a}") for a in range(PASSES)]
        w2_codes = kept([P, PASSES, 2 * H], U8, "w2c")
        w2_planes = kept([P, PASSES, H], U8, "w2s")
        w3_raw = kept([P, PACK, N], F32, "w3raw")
        w3_codes = kept([P, N], U32, "w3c")
        w3_scales = kept([P, N], U8, "w3s")
        w4_codes = kept([P, N], I32, "w4c")
        w4_planes = kept([P, N], U8, "w4s")
        tare_t = kept([P, PACK], F32, "tare_t")
        pages = [kept([P, T2], F32, f"page{t}") for t in range(PACK)]
        sea = [kept([P, t1 - t0, j1 - j0], F32, f"sea{n}") for n, (t0, t1, j0, j1) in enumerate(MADE)]
        wg = [kept([P, j1 - j0], F32, f"wg{n}") for n, (t, j0, j1) in enumerate(PLACED)]
        hf = kept([P, PACK, S], F32, "hf")

        season_v = season.rearrange("(p t) j -> p t j", t=PACK)
        wgs_v = wgs.rearrange("(m t) j -> t m j", t=PACK)
        page_v = page0.rearrange("(p t) m -> t p m", t=PACK)
        out1_v = out_1.rearrange("(p t) m -> t p m", t=PACK)

        def load_season(n):
            t0, t1, j0, j1 = MADE[n]
            nc.sync.dma_start(out=sea[n][:], in_=season_v[:, t0:t1, j0:j1])

        def load_wgs(n):
            t, j0, j1 = PLACED[n]
            for q in (0, 2, 1, 3):
                nc.sync.dma_start(out=wg[n][QUAD * q : QUAD * (q + 1), :], in_=wgs_v[t][:, j0:j1])

        def load_page(t):
            nc.sync.dma_start(out=pages[t][:], in_=page_v[t])

        with tc.tile_pool(name="head", bufs=1) as head:
            tw = [head.tile([P, T], I32, name=f"tw{a}", align_bytes=64) for a in range(PASSES)]
            w1_raw = [head.tile([P, PACK, H], F32, name=f"w1raw{a}", align_bytes=64) for a in range(PASSES)]
            w1_bf = [head.tile([P, H, PACK], BF16, name=f"w1bf{a}", align_bytes=64) for a in range(PASSES)]
            ts = head.tile([P, T], U8, name="ts", align_bytes=64)
            w2s_raw = head.tile([P, PASSES, H], U8, name="w2sraw", align_bytes=64)
            w2_raw = head.tile([P, PASSES, 2 * H], U8, name="w2raw", align_bytes=64)

            nc.vector.memset(w2s_raw[:].rearrange("p a c -> p (a c)").bitcast(I32), 0)
            nc.vector.memset(ts[QUAD : 2 * QUAD, :].bitcast(I32), 0)
            nc.vector.memset(ts[2 * QUAD : P, :].bitcast(I32), 0)
            nc.vector.memset(v_scales[:].rearrange("p a j -> p (a j)").bitcast(I32), 0)
            nc.vector.memset(w4_planes[:].bitcast(I32), 0)

            w1_v = w1.rearrange("(a p i) c -> a p i c", a=PASSES, i=PACK)
            tw_v = tab_words.rearrange("a p t i -> a p (t i)")
            nc.sync.dma_start(idx[:], offs)
            nc.sync.dma_start(out=ts[0:QUAD, :].bitcast(I32), in_=tab_scales.rearrange("a q t -> q a t").bitcast(I32))
            nc.sync.dma_start(out=w2_raw[:].bitcast(I32), in_=w2_words.rearrange("a p c -> p a c").bitcast(I32))
            for a in range(PASSES):
                nc.sync.dma_start(out=w1_raw[a][:], in_=w1_v[a])
            for a in range(PASSES):
                nc.sync.dma_start(out=tw[a][:], in_=tw_v[a].bitcast(I32))
            for q in range(QUADS):
                nc.gpsimd.dma_start(
                    out=w2s_raw[QUAD * q : QUAD * q + ROWS, :, :].bitcast(I32),
                    in_=w2_scales[:, ROWS * q : ROWS * (q + 1), :].rearrange("a r c -> r a c").bitcast(I32),
                )

            load_season(0)
            nc.sync.dma_start(idx2[:], offs2)
            load_season(1)
            load_wgs(0)
            load_page(0)
            load_wgs(1)
            nc.sync.dma_start(idx3[:], offs3)
            nc.sync.dma_start(out=tare_t[:], in_=tare.rearrange("(p t) -> p t", t=PACK))
            load_season(2)
            load_wgs(2)
            load_page(1)
            load_wgs(3)
            load_page(2)
            load_season(3)
            nc.sync.dma_start(out=w3_raw[:], in_=w3.rearrange("(p i) c -> p i c", i=PACK))
            nc.sync.dma_start(out=w4_codes[:], in_=w4_words.rearrange("a p c i -> p (a c i)").bitcast(I32))
            for q in range(QUADS):
                nc.sync.dma_start(
                    out=w4_planes[QUAD * q : QUAD * q + ROWS, :].bitcast(I32),
                    in_=w4_scales[0, ROWS * q : ROWS * (q + 1), :].bitcast(I32),
                )
            load_wgs(4)
            load_page(3)

            nc.vector.tensor_copy(v_rows[:], ts[:].indirect(idx[:]))
            for q in range(QUADS):
                nc.gpsimd.dma_start(
                    out=v_scales[QUAD * q : QUAD * q + ROWS, :, :].rearrange("p a j -> p (a j)").bitcast(I32),
                    in_=v_rows[PASSES * ROWS * q : PASSES * ROWS * (q + 1), :].bitcast(I32),
                )
            for a in range(PASSES):
                nc.vector.tensor_copy(
                    out=w2_codes[:, a, :].bitcast(U16).rearrange("p (t m) -> p t m", t=PACK),
                    in_=w2_raw[:, a, :].bitcast(U16).rearrange("p (m t) -> p t m", t=PACK),
                )
            nc.vector.tensor_copy(
                out=w2_planes[:].rearrange("p a (t m) -> p a t m", t=PACK),
                in_=w2s_raw[:].rearrange("p a (m t) -> p a t m", t=PACK),
            )
            for a in range(PASSES):
                nc.scalar.copy(
                    out=w1_bf[a][:].rearrange("p (t m) i -> p m t i", t=PACK),
                    in_=w1_raw[a][:].rearrange("p i (m t) -> p m t i", t=PACK),
                )
                nc.vector.quantize_mx(
                    out=w1_codes[a][:].bitcast(FP8X4), scales=w1_scales[a][:],
                    in_=w1_bf[a][:].rearrange("p c i -> p (c i)"),
                )
            for a in range(PASSES):
                for h in range(HALVES):
                    nc.vector.tensor_copy(
                        v_words[a][:, h * HALF : (h + 1) * HALF],
                        tw[a][:].bitcast(U32).indirect(entries(idx, h * HALF, (h + 1) * HALF)),
                    )

        tail = ctx.enter_context(tc.tile_pool(name="tail", bufs=1))

        def late(shape, dtype, name):
            return tail.tile(shape, dtype, name=name, tag=name, align_bytes=64)

        page_pairs = [late([P, 2, CHUNK, 2], BF16, f"pp{c}") for c in range(CHUNKS)]
        page_codes = [late([P, CHUNK], U32, f"pc{c}") for c in range(CHUNKS)]
        page_scales = late([P, T2], U8, "ps")
        x_pairs = [late([P, 2, HALF, 2], BF16, f"xp{h}") for h in range(HALVES)]
        ys = [[late([P, HALF], F32, f"y{h}{n}") for n in range(NT)] for h in range(HALVES)]

        def interleave(grouped, rows):
            nc.scalar.copy(
                out=grouped.rearrange("p (c i) t -> p c t i", i=4), in_=rows.rearrange("p t (c i) -> p c t i", i=4)
            )

        def prepare_w3():
            w3_bf = kept([P, N, PACK], BF16, "w3bf", slot="big1")
            interleave(w3_bf[:], w3_raw[:])
            for c0, c1 in W3_CUTS:
                nc.vector.quantize_mx(
                    out=w3_codes[:, c0:c1].bitcast(FP8X4), scales=w3_scales[:, c0:c1],
                    in_=w3_bf[:, c0:c1, :].rearrange("p c i -> p (c i)"),
                )

        def negate_tare():
            neg = kept([P, PACK], F32, "neg_tare", slot="sea2")
            nc.vector.tensor_scalar(neg[:], tare_t[:], -1.0, None, ALU.mult)
            return neg

        def product_pass(t, h, a, banks):
            cols = slice(P * t, P * (t + 1))
            jc = slice(HALF * h, HALF * (h + 1))
            moving = dict(
                rhs=v_words[a][:, jc].bitcast(FP8X4), rhs_scale=v_scales[:, a, jc],
                start=(a == 0), stop=(a == PASSES - 1),
            )
            nc.tensor.matmul_mx(
                out=banks[1][:], lhsT=w2_codes[:, a, 2 * P * t : 2 * P * (t + 1)].bitcast(FP4X4),
                lhsT_scale=w2_planes[:, a, cols], **moving,
            )
            nc.tensor.matmul_mx(
                out=banks[0][:], lhsT=w1_codes[a][:, cols].bitcast(FP8X4), lhsT_scale=w1_scales[a][:, cols], **moving
            )

        def products(groups):
            banks = [
                (
                    psum.tile([P, HALF], F32, name="a_ps", tag="held", bufs=HELD_BANKS),
                    psum.tile([P, HALF], F32, name="b_ps", tag="passing", bufs=PASSING_BANKS),
                )
                for group in groups
            ]
            for (t, h), pair in zip(groups, banks):
                product_pass(t, h, 0, pair)
            sums = []
            for (t, h), pair in zip(groups, banks):
                product_pass(t, h, 1, pair)
                b_sb = ring.tile([P, HALF], F32, name="b_sb")
                nc.scalar.copy(out=b_sb[:], in_=pair[1][:])
                sums.append((pair[0], b_sb))
            return sums

        def larger(sums, slot):
            big = kept([P, len(sums) * HALF], F32, "big", slot=slot)
            for i, (a_ps, b_sb) in enumerate(sums):
                nc.vector.tensor_tensor(big[:, i * HALF : (i + 1) * HALF], a_ps[:], b_sb[:], ALU.max)
            return big

        def seasoned(n, big):
            t0, t1, j0, j1 = MADE[n]
            nc.vector.tensor_tensor(
                hf[:, t0:t1, j0:j1], big[:].rearrange("p (t j) -> p t j", t=t1 - t0), sea[n][:], ALU.mult
            )

        def place(n):
            t, j0, j1 = PLACED[n]
            nc.vector.tensor_tensor(pages[t][:].indirect(entries(idx2, j0, j1)), hf[:, t, j0:j1], wg[n][:], ALU.mult)

        def round_page(t, chunks):
            for c in chunks:
                nc.scalar.copy(out=page_pairs[c][:, t // 2, :, t % 2], in_=pages[t][:, c * CHUNK : (c + 1) * CHUNK])

        def read_page(t, halves, neg_tare):
            got = tail.tile([P, len(halves) * HALF], F32, name="got", bufs=3, align_bytes=64)
            nc.vector.tensor_copy(
                got[:], pages[t][:].indirect(entries(idx3, halves[0] * HALF, (halves[-1] + 1) * HALF))
            )
            nc.scalar.activation(got[:], got[:], ACT.Abs)
            for i, h in enumerate(halves):
                nc.scalar.activation(
                    x_pairs[h][:, t // 2, :, t % 2], got[:, i * HALF : (i + 1) * HALF], ACT.Identity,
                    bias=neg_tare[:, t : t + 1],
                )

        def quantise(name, grouped):
            codes = late([P, HALF], U32, name + "c")
            scales = late([P, HALF], U8, name + "s")
            nc.vector.quantize_mx(out=codes[:].bitcast(FP8X4), scales=scales[:], in_=grouped)
            return codes, scales

        def weave(pairs, on_scalar):
            pair = U32 if on_scalar else I32
            woven = tail.tile([P, HALF, 2], pair, name="woven", bufs=3, align_bytes=64)
            move = nc.scalar.copy if on_scalar else nc.vector.tensor_copy
            move(
                out=woven[:],
                in_=pairs[:].rearrange("p u m e -> p (u m e)").bitcast(pair).rearrange("p (u m) -> p m u", u=2),
            )
            return woven[:].rearrange("p m u -> p (m u)").bitcast(BF16)

        def round_h(h):
            h_bf = late([P, HALF, PACK], BF16, f"hbf{h}")
            interleave(h_bf[:], hf[:, :, h * HALF : (h + 1) * HALF])
            return h_bf

        def tanh_part(h, h_bf):
            codes, scales = quantise(f"hq{h}", h_bf[:].rearrange("p j t -> p (j t)"))
            for n in range(NT):
                cols = slice(P * n, P * (n + 1))
                f_ps = psum.tile([P, HALF], F32, name="f_ps", tag="passing", bufs=PASSING_BANKS)
                nc.tensor.matmul_mx(
                    out=f_ps[:], lhsT=w4_codes[:, cols].bitcast(FP8X4), lhsT_scale=w4_planes[:, cols],
                    rhs=codes[:].bitcast(FP8X4), rhs_scale=scales[:], start=True, stop=True,
                )
                nc.scalar.activation(ys[h][n][:], f_ps[:], ACT.Tanh)

        def finish(h, codes, scales):
            for n in range(NT):
                cols = slice(P * n, P * (n + 1))
                e_ps = psum.tile([P, HALF], F32, name="e_ps", tag="held", bufs=HELD_BANKS)
                nc.tensor.matmul_mx(
                    out=e_ps[:], lhsT=w3_codes[:, cols].bitcast(FP8X4), lhsT_scale=w3_scales[:, cols],
                    rhs=codes[:].bitcast(FP8X4), rhs_scale=scales[:], start=True, stop=True,
                )
                nc.vector.tensor_tensor(ys[h][n][:], e_ps[:], ys[h][n][:], ALU.subtract)
                nc.sync.dma_start(out=out_0[cols, HALF * h : HALF * (h + 1)], in_=ys[h][n][:])

        def planes(c, woven):
            cols = slice(c * CHUNK, (c + 1) * CHUNK)
            nc.vector.quantize_mx(out=page_codes[c][:].bitcast(FP8X4), scales=page_scales[:, cols], in_=woven)
            nc.sync.dma_start(
                out=out_2.rearrange("g p m t -> p (g m t)").bitcast(I32)[:, cols], in_=page_codes[c][:].bitcast(I32)
            )

        def page_out(t):
            nc.sync.dma_start(out=out1_v[t], in_=pages[t][:])
            round_page(t, range(CHUNKS))

        sums = products([(0, h) for h in range(HALVES)])
        for t in range(1, PACK):
            for h in range(HALVES):
                sums.extend(products([(t, h)]))
        big0 = larger(sums[0:1], "big0")
        big1 = larger(sums[1:2], "big1")
        seasoned(0, big0)
        seasoned(1, big1)
        place(0)
        big2 = larger(sums[2:4], "wg0")
        place(1)
        seasoned(2, big2)
        neg_tare = negate_tare()
        page_out(0)
        read_page(0, (0, 1), neg_tare)
        place(2)
        big3 = larger(sums[4:8], "wg1")
        page_out(1)
        read_page(1, (0,), neg_tare)
        seasoned(3, big3)
        h_bfs = [round_h(h) for h in range(HALVES)]
        read_page(1, (1,), neg_tare)
        place(3)
        page_out(2)
        read_page(2, (0, 1), neg_tare)
        for h in range(HALVES):
            tanh_part(h, h_bfs[h])
        prepare_w3()
        place(4)
        last = PACK - 1
        nc.sync.dma_start(out=out1_v[last], in_=pages[last][:])
        round_page(last, (0,))
        read_page(last, (0,), neg_tare)
        read_page(last, (1,), neg_tare)
        planes(0, weave(page_pairs[0], False))
        xq = [quantise(f"xq{h}", weave(x_pairs[h], False)) for h in range(HALVES)]
        round_page(last, (1, 2))
        woven2 = weave(page_pairs[2], True)
        round_page(last, (3,))
        woven3 = weave(page_pairs[3], True)
        finish(0, *xq[0])
        planes(1, weave(page_pairs[1], False))
        planes(2, woven2)
        finish(1, *xq[1])
        planes(3, woven3)
        for q in range(QUADS):
            nc.sync.dma_start(
                out=out_3[0, ROWS * q : ROWS * (q + 1), :].bitcast(I32),
                in_=page_scales[QUAD * q : QUAD * q + ROWS, :].bitcast(I32),
            )
